import numpy as np
import ml_dtypes


def mxq(x, axis, fmt="e4m3"):
    dtype, down = {"e4m3": (ml_dtypes.float8_e4m3fn, 7), "e5m2": (ml_dtypes.float8_e5m2, 14)}[fmt]
    v = np.moveaxis(np.asarray(x, np.float32).astype(ml_dtypes.bfloat16).astype(np.float64), axis, -1)
    blocks = v.reshape(v.shape[:-1] + (-1, 32))
    amax = np.abs(blocks).max(-1, keepdims=True)
    byte = np.maximum(np.where(amax > 0, np.frexp(amax)[1] - 1 + 127, 0) - down, 1)
    scale = np.exp2(byte - 127.0)
    codes = (blocks / scale).astype(np.float32).astype(dtype).astype(np.float64)
    return np.moveaxis((codes * scale).reshape(v.shape), -1, axis)


WIDE = False


def mx_kscale(k):
    if not WIDE:
        return np.ones(k)
    levels = np.array([10, -10, 5, -5, 0])
    if k % 512:
        return np.exp2(np.random.permutation(np.resize(levels, k // 32))).repeat(32)
    a = np.empty((k // 512, 16))
    for p in range(k // 512):
        a[p, :8] = np.random.permutation(np.resize(levels, 8))
        for g in range(8):
            far = levels[np.abs(levels - a[p, g]) >= 10]
            a[p, g + 8] = far[np.random.randint(len(far))]
    return np.exp2(a.ravel()).repeat(32)


BF16 = ml_dtypes.bfloat16


def bf(x):
    return np.asarray(x, np.float32).astype(BF16)


def f64(x):
    return np.asarray(x).astype(np.float64)


B, YY, XX, F, E = 8, 6, 8, 512, 1024
T3 = 3
YP, XP = YY + T3 - 1, XX + T3 - 1
G = 3 * F


def sigmoid(v):
    return 1.0 / (1.0 + np.exp(-v))


def draw0():
    s, t = mx_kscale(F), mx_kscale(F)
    return {
        "h": bf(np.random.standard_normal((B, YP, XP, F)) * s),
        "c": bf(np.random.standard_normal((B, YY, XX, F))),
        "wh": bf(np.random.standard_normal((T3, T3, F, G)) * (0.35 / np.sqrt(F)) / s[:, None]),
        "peep_f": bf(np.random.standard_normal((YY, XX, F)) * 0.5),
        "peep_o": bf(np.random.standard_normal((YY, XX, F)) * 0.5),
        "gain": bf((1.0 + 0.1 * np.random.standard_normal(F)) * t),
        "wo": bf(np.random.standard_normal((F, E)) * (2.0 / np.sqrt(F)) / t[:, None]),
    }


def tap(hq, whq, dy, dx, rows, cols):
    window = hq[:, dy:dy + rows, dx:dx + cols, :]
    return window @ whq[dy, dx]


def nine_taps(h, wh, rows, cols):
    hq = mxq(h, 3, "e4m3")
    whq = mxq(wh, 2, "e4m3")
    return (
        tap(hq, whq, 0, 0, rows, cols)
        + tap(hq, whq, 0, 1, rows, cols)
        + tap(hq, whq, 0, 2, rows, cols)
        + tap(hq, whq, 1, 0, rows, cols)
        + tap(hq, whq, 1, 1, rows, cols)
        + tap(hq, whq, 1, 2, rows, cols)
        + tap(hq, whq, 2, 0, rows, cols)
        + tap(hq, whq, 2, 1, rows, cols)
        + tap(hq, whq, 2, 2, rows, cols)
    )


def core(h, c, wh, peep_f, peep_o, gain, wo):
    h, c, wh = f64(h), f64(c), f64(wh)
    peep_f, peep_o, gain, wo = f64(peep_f), f64(peep_o), f64(gain), f64(wo)
    rows, cols = c.shape[1], c.shape[2]
    pre = nine_taps(h, wh, rows, cols)
    pf, pg, po = np.split(pre, 3, axis=-1)
    f = sigmoid(pf + peep_f[None, :, :, :] * c)
    c_new = f * c + (1.0 - f) * np.tanh(pg)
    o = sigmoid(po + peep_o[None, :, :, :] * c_new)
    hg = gain * (o * np.tanh(c_new))
    y = mxq(hg, 3, "e4m3") @ mxq(wo, 0, "e4m3")
    return y, c_new


def e4m3fn_bytes(y):
    return np.clip(np.asarray(y, np.float64), -448.0, 448.0).astype(np.float32).astype(ml_dtypes.float8_e4m3fn).view(np.uint8)


def e4m3fn_values(b):
    return np.asarray(b, np.uint8).view(ml_dtypes.float8_e4m3fn).astype(np.float64)


def setup_inputs():
    d = draw0()
    x0 = np.asarray(d['wh']).astype(np.float64)
    s = (np.max(np.abs(x0), axis=(0, 1, 3), keepdims=True) / 448.0).astype(np.float32)
    out = {}
    for k, v in d.items():
        if k == 'wh':
            out['wh_bytes'] = e4m3fn_bytes(x0 / s.astype(np.float64))
            out['wh_scale'] = s
        else:
            out[k] = v
    return out


def reference(h, c, wh_bytes, wh_scale, peep_f, peep_o, gain, wo):
    return core(h, c, e4m3fn_values(wh_bytes) * wh_scale.astype(np.float64), peep_f, peep_o, gain, wo)

@@ -1,0 +1,342 @@
+from contextlib import ExitStack
+
+import concourse.mybir as mybir
+from concourse.masks import make_identity
+
+F32 = mybir.dt.float32
+BF16 = mybir.dt.bfloat16
+I32 = mybir.dt.int32
+U8 = mybir.dt.uint8
+FP8 = mybir.dt.float8_e4m3fn
+FP8X4 = mybir.dt.float8_e4m3fn_x4
+ACT = mybir.ActivationFunctionType
+ALU = mybir.AluOpType
+
+B, YY, XX, F, E = 8, 6, 8, 512, 1024
+YP, XP = YY + 2, XX + 2
+P = 128
+PACK = 4
+TAPS = 9
+POS = YY * XX
+TOK = B * POS
+MT = TOK // P
+HALO = B * YP * XP
+HT = HALO // P
+
+FLOPS = 2 * TOK * F * (TAPS * 3 * F + E)
+
+HALF = F // 2
+UNITS = [[(gate, tap, 0, F)] for gate in range(2) for tap in range(TAPS)]
+O_STRIPS = [(2, tap, half * HALF, HALF) for half in range(2) for tap in range(TAPS)]
+O_UNITS = [O_STRIPS[i:i + 2] for i in range(0, 16, 2)] + [O_STRIPS[16:17], O_STRIPS[17:18]]
+ALL_UNITS = UNITS + O_UNITS
+GROUPS = [[0], [1], [2, 3], [4, 5], [6, 7], [8, 9], [10, 11], [12, 13], [14, 15], [16, 17], [18, 19], [20, 21], [22, 23], [24, 25], [26], [27]]
+VECTOR_WIDENS = {0}
+TENSOR_INTERLEAVES = set()
+SCALAR_INTERLEAVES = {24}
+WO_ON_TENSOR = False
+LEAD = 2
+
+
+def interleave_views(dst, src):
+    return (dst.rearrange("p (c i) t -> p c t i", i=4), src.rearrange("p t (c i) -> p c t i", i=4))
+
+
+def tile_peepholeconvlstmninetap_kernel(tc, h, c, wh_bytes, wh_scale, peep_f, peep_o, gain, wo, out_0, out_1):
+    nc = tc.nc
+    with ExitStack() as ctx:
+        keep = ctx.enter_context(tc.tile_pool(name="keep", bufs=1))
+        work = ctx.enter_context(tc.tile_pool(name="work", bufs=3))
+        psum = ctx.enter_context(tc.psum_pool(name="psum", bufs=1))
+        ctx.enter_context(tc.manual_schedule())
+
+        units = ALL_UNITS
+        width = [sum(s[3] for s in u) for u in units]
+        group_of = {k: gi for gi, g in enumerate(GROUPS) for k in g}
+        start_in_group = {k: sum(width[j] for j in g if j < k) for g in GROUPS for k in g}
+        group_width = [sum(width[k] for k in g) for g in GROUPS]
+
+        wscale = keep.tile([P, PACK], F32, name="wscale")
+        nc.sync.dma_start(out=wscale[:], in_=wh_scale.rearrange("a b (p t) o -> p (a b t o)", t=PACK))
+        wbytes = [keep.tile([P, PACK, w], U8, name="wbytes%d" % gi) for gi, w in enumerate(group_width)]
+
+        def load_w(k):
+            at = start_in_group[k]
+            for gate, tap, c0, w in units[k]:
+                src = wh_bytes[tap // 3, tap % 3].rearrange("(p t) n -> p t n", t=PACK)
+                nc.sync.dma_start(out=wbytes[group_of[k]][:, :, at:at + w], in_=src[:, :, gate * F + c0:gate * F + c0 + w])
+                at = at + w
+
+        def load_peep(dst, src):
+            rows = src.rearrange("i j f -> (i j) f")
+            for m in range(MT):
+                p0 = 0
+                while p0 < P:
+                    r0 = (m * P + p0) % POS
+                    n = min(POS - r0, P - p0)
+                    nc.sync.dma_start(out=dst[p0:p0 + n, m, :], in_=rows[r0:r0 + n, :])
+                    p0 = p0 + n
+
+        load_w(0)
+        load_w(1)
+        h_rows = h.rearrange("b i j f -> (b i j) f").rearrange("(m p) f -> p m f", p=P)
+        h_pairs = [(m0, min(2, HT - m0)) for m0 in range(0, HT, 2)]
+        h_raw = []
+        for m0, n in h_pairs:
+            t = keep.tile([P, n, F], BF16, name="h_raw%d" % m0)
+            nc.sync.dma_start(out=t[:], in_=h_rows[:, m0:m0 + n, :])
+            h_raw.append(t)
+        for k in range(2, 6):
+            load_w(k)
+        wo_raw = keep.tile([P, PACK, E], BF16, name="wo_raw")
+        nc.sync.dma_start(out=wo_raw[:], in_=wo.rearrange("(p t) e -> p t e", t=PACK))
+        for k in range(6, 12):
+            load_w(k)
+        c_sb = keep.tile([P, MT, F], BF16, name="c_sb")
+        nc.sync.dma_start(out=c_sb[:], in_=c.rearrange("b i j f -> (b i j) f").rearrange("(m p) f -> p m f", p=P))
+        pf_sb = keep.tile([P, MT, F], BF16, name="pf_sb")
+        load_peep(pf_sb, peep_f)
+        for k in range(12, 20):
+            load_w(k)
+        gain_sb = keep.tile([P, F], BF16, name="gain_sb")
+        nc.sync.dma_start(out=gain_sb[:], in_=gain.partition_broadcast(P))
+        po_sb = keep.tile([P, MT, F], BF16, name="po_sb")
+        load_peep(po_sb, peep_o)
+        for k in range(20, len(units)):
+            load_w(k)
+
+        ident = keep.tile([P, P], F32, name="ident")
+        make_identity(nc, ident[:])
+        ident_b = keep.tile([P, P], BF16, name="ident_b")
+        make_identity(nc, ident_b[:])
+        h_scales = keep.tile([P, HALO], U8, name="h_scales", align_bytes=64)
+        nc.vector.memset(h_scales[:].bitcast(I32), 0)
+
+        planes = {}
+
+        def widen(gi, t):
+            if gi not in planes:
+                planes[gi] = work.tile([P, PACK, group_width[gi]], BF16, name="planes", tag="planes", bufs=4)
+            src = wbytes[gi][:, t, :].bitcast(FP8)
+            if GROUPS[gi][0] in VECTOR_WIDENS:
+                nc.vector.tensor_scalar(out=planes[gi][:, t, :], in0=src, scalar1=wscale[:, t:t + 1], scalar2=None, op0=ALU.mult)
+            else:
+                nc.scalar.activation(out=planes[gi][:, t, :], in_=src, func=ACT.Copy, scale=wscale[:, t:t + 1])
+
+        widen_at = {}
+        for gi, g in enumerate(GROUPS):
+            for t in range(PACK):
+                widen_at.setdefault(max(-1, g[0] - LEAD - len(g) + 1 + t * len(g) // PACK), []).append((gi, t))
+        il = {}
+        acc = {}
+
+        def tensor_interleave(dst, src, n):
+            for b0 in range(0, n, 2 * P):
+                tp = psum.tile([P, 2 * F], BF16, name="tp", tag="tp", bufs=2)
+                for j in range(2):
+                    nc.tensor.matmul(out=tp[:, j * F:(j + 1) * F], lhsT=ident_b[:],
+                                     rhs=src[:, :, b0 + j * P:b0 + (j + 1) * P].rearrange("p t n -> p n t"), start=True, stop=True)
+                nc.scalar.copy(out=dst[:, b0 * PACK:(b0 + 2 * P) * PACK], in_=tp[:])
+
+        def interleave(k):
+            at = start_in_group[k]
+            il[k] = work.tile([P, width[k], PACK], BF16, name="il", tag="il", bufs=4, align_bytes=64)
+            src = planes[group_of[k]][:, :, at:at + width[k]]
+            if k in TENSOR_INTERLEAVES:
+                tensor_interleave(il[k][:].rearrange("p n t -> p (n t)"), src, width[k])
+                return
+            dst, src = interleave_views(il[k][:], src)
+            if k in SCALAR_INTERLEAVES:
+                nc.scalar.copy(out=dst, in_=src)
+            else:
+                nc.vector.tensor_copy(out=dst, in_=src)
+
+        for gi, t in widen_at[-1]:
+            widen(gi, t)
+        interleave(0)
+
+        h_il = keep.tile([P, HALO * PACK], BF16, name="h_il", align_bytes=64)
+        h_codes = keep.tile([P, HALO], I32, name="h_codes", align_bytes=64)
+        for (m0, n), raw in zip(h_pairs, h_raw):
+            tp = psum.tile([P, 2, 2, P], F32, name="tp", tag="tp", bufs=2)
+            for m in range(n):
+                words = raw[:, m, :].bitcast(F32)
+                for u in range(2):
+                    nc.tensor.transpose(tp[:, m, u, :], words[:, u:F // 2:2], ident[:])
+            dst = h_il[:, m0 * P * PACK:(m0 + n) * P * PACK].bitcast(F32).rearrange("p (m r u) -> p m r u", m=n, u=2)
+            nc.vector.tensor_copy(out=dst, in_=tp[:, 0:n, :, :].rearrange("p m u r -> p m r u"))
+        for c0, c1 in ((0, 512), (512, HALO)):
+            nc.vector.quantize_mx(out=h_codes[:, c0:c1].bitcast(FP8X4), scales=h_scales[:, c0:c1],
+                                  in_=h_il[:, c0 * PACK:c1 * PACK])
+
+        win_codes = keep.tile([P, TAPS, TOK], I32, name="win_codes", align_bytes=64)
+        win_scales = keep.tile([P, TAPS, TOK], U8, name="win_scales", align_bytes=64)
+        dx_scales = keep.tile([P, 3, B * YP * XX], U8, name="dx_scales", align_bytes=64)
+
+        def shift_scales():
+            rows = h_scales[:].rearrange("p (r j) -> p r j", j=XP)
+            for dx in range(3):
+                nc.vector.tensor_copy(out=dx_scales[:, dx, :].rearrange("p (r j) -> p r j", j=XX), in_=rows[:, :, dx:dx + XX])
+
+        def window_scales(dy):
+            src = dx_scales[:].rearrange("p d n -> p (d n)").bitcast(I32).rearrange("p (q w) -> p q w", w=YP * XX // 4)
+            dst = win_scales[:, 3 * dy:3 * dy + 3, :].rearrange("p d n -> p (d n)").bitcast(I32)
+            nc.vector.tensor_copy(out=dst.rearrange("p (q w) -> p q w", w=POS // 4),
+                                  in_=src[:, :, dy * XX // 4:dy * XX // 4 + POS // 4])
+
+        def window_codes(tap):
+            dy, dx = tap // 3, tap % 3
+            src = h_codes[:].rearrange("p (b i j) -> p b i j", i=YP, j=XP)
+            nc.vector.tensor_copy(out=win_codes[:, tap, :].rearrange("p (b i j) -> p b i j", i=YY, j=XX),
+                                  in_=src[:, :, dy:dy + YY, dx:dx + XX])
+
+        def quantise_multiply(k):
+            codes = work.tile([P, width[k]], I32, name="codes", tag="codes", bufs=4, align_bytes=64)
+            scales = work.tile([P, width[k]], U8, name="scales", tag="scales", bufs=4, align_bytes=64)
+            nc.vector.quantize_mx(out=codes[:].bitcast(FP8X4), scales=scales[:], in_=il[k][:].rearrange("p n t -> p (n t)"))
+            at = 0
+            for gate, tap, c0, w in units[k]:
+                for m in range(MT):
+                    if tap == 0:
+                        acc[gate, m, c0] = psum.tile([P, w], F32, name="acc", tag="acc", bufs=6)
+                    nc.tensor.matmul_mx(out=acc[gate, m, c0][:], lhsT=win_codes[:, tap, m * P:(m + 1) * P].bitcast(FP8X4),
+                                        lhsT_scale=win_scales[:, tap, m * P:(m + 1) * P],
+                                        rhs=codes[:, at:at + w].bitcast(FP8X4), rhs_scale=scales[:, at:at + w],
+                                        start=(tap == 0), stop=(tap == TAPS - 1))
+                at = at + w
+
+        wo_il = keep.tile([P, E, PACK], BF16, name="wo_il", align_bytes=64)
+        wo_codes = keep.tile([P, E], I32, name="wo_codes", align_bytes=64)
+        wo_scales = keep.tile([P, E], U8, name="wo_scales", align_bytes=64)
+
+        def wo_interleave(half):
+            cols = slice(half * F, (half + 1) * F)
+            if WO_ON_TENSOR:
+                tensor_interleave(wo_il[:, cols, :].rearrange("p n t -> p (n t)"), wo_raw[:, :, cols], F)
+                return
+            dst, src = interleave_views(wo_il[:, cols, :], wo_raw[:, :, cols])
+            nc.scalar.copy(out=dst, in_=src)
+
+        def wo_quantise(half):
+            cols = slice(half * F, (half + 1) * F)
+            nc.vector.quantize_mx(out=wo_codes[:, cols].bitcast(FP8X4), scales=wo_scales[:, cols],
+                                  in_=wo_il[:, cols, :].rearrange("p n t -> p (n t)"))
+
+        gate_in = keep.tile([P, MT, F], F32, name="gate_in")
+        kept = keep.tile([P, MT, F], F32, name="kept")
+        cand = keep.tile([P, MT, F], F32, name="cand")
+        c_new = keep.tile([P, MT, F], F32, name="c_new")
+        c_half = keep.tile([P, MT, F], BF16, name="c_half")
+
+        def flat(t):
+            return t[:].rearrange("p m f -> p (m f)")
+
+        def peep_f_term():
+            nc.vector.tensor_tensor(out=flat(gate_in), in0=flat(pf_sb), in1=flat(c_sb), op=ALU.mult)
+
+        def halve_c():
+            nc.vector.tensor_scalar(out=flat(c_half), in0=flat(c_sb), scalar1=0.5, scalar2=None, op0=ALU.mult)
+
+        def add_pre(gate, m, c0, w):
+            nc.vector.tensor_tensor(out=gate_in[:, m, c0:c0 + w], in0=acc[gate, m, c0][:], in1=gate_in[:, m, c0:c0 + w], op=ALU.add)
+
+        def tanh_f():
+            nc.scalar.activation(out=flat(gate_in), in_=flat(gate_in), func=ACT.Tanh, scale=0.5)
+
+        def keep_term():
+            nc.vector.scalar_tensor_tensor(out=flat(kept), in0=flat(gate_in), scalar=1.0, in1=flat(c_half), op0=ALU.add, op1=ALU.mult)
+
+        def tanh_g():
+            for m in range(MT):
+                nc.scalar.activation(out=cand[:, m, :], in_=acc[1, m, 0][:], func=ACT.Tanh)
+
+        def cand_term():
+            nc.vector.scalar_tensor_tensor(out=flat(cand), in0=flat(gate_in), scalar=-1.0, in1=flat(cand), op0=ALU.add, op1=ALU.mult)
+
+        def cell():
+            nc.vector.scalar_tensor_tensor(out=flat(c_new), in0=flat(cand), scalar=-0.5, in1=flat(kept), op0=ALU.mult, op1=ALU.add)
+            nc.sync.dma_start(out=out_1.rearrange("b i j f -> (b i j) f").rearrange("(m p) f -> p m f", p=P), in_=c_new[:])
+
+        def peep_o_term():
+            nc.vector.tensor_tensor(out=flat(gate_in), in0=flat(c_new), in1=flat(po_sb), op=ALU.mult)
+
+        def tanh_c():
+            nc.scalar.activation(out=flat(cand), in_=flat(c_new), func=ACT.Tanh)
+
+        def gain_term():
+            for m in range(MT):
+                nc.vector.scalar_tensor_tensor(out=cand[:, m, :], in0=cand[:, m, :], scalar=0.5, in1=gain_sb[:], op0=ALU.mult, op1=ALU.mult)
+
+        def add_f():
+            for m in range(MT):
+                add_pre(0, m, 0, F)
+
+        hg = keep.tile([P, MT, F], BF16, name="hg")
+
+        def add_o_first():
+            for m in range(MT):
+                add_pre(2, m, 0, HALF)
+
+        def tanh_o_first():
+            nc.scalar.activation(out=gate_in[:, :, 0:HALF], in_=gate_in[:, :, 0:HALF], func=ACT.Tanh, scale=0.5)
+
+        def hg_first():
+            nc.vector.scalar_tensor_tensor(out=hg[:, :, 0:HALF], in0=gate_in[:, :, 0:HALF], scalar=1.0, in1=cand[:, :, 0:HALF], op0=ALU.add, op1=ALU.mult)
+
+        after_il = {0: [shift_scales, lambda: window_codes(0), lambda: window_scales(0)], 3: [lambda: window_scales(1)], 6: [lambda: window_scales(2)],
+            7: [peep_f_term], 8: [halve_c], 11: [add_f], 14: [keep_term], 20: [cand_term], 21: [cell], 22: [peep_o_term], 23: [gain_term], 25: [add_o_first], 27: [hg_first]}
+        after_q = {12: [tanh_f], 18: [tanh_g], 21: [tanh_c], 25: [tanh_o_first], 26: [lambda: wo_interleave(0), lambda: wo_interleave(1)]}
+        for k in range(len(units)):
+            for gi, t in widen_at.get(k, []):
+                widen(gi, t)
+            early = TENSOR_INTERLEAVES | SCALAR_INTERLEAVES
+            if k + 1 in early:
+                interleave(k + 1)
+            if k >= 1 and k not in early:
+                interleave(k)
+            if 1 <= k < TAPS:
+                window_codes(k)
+            for step in after_il.get(k, []):
+                step()
+            if k >= 1:
+                quantise_multiply(k - 1)
+            for step in after_q.get(k, []):
+                step()
+        quantise_multiply(len(units) - 1)
+
+        y_rows = out_0.rearrange("b i j e -> (b i j) e")
+        last0, last_w = HALF, HALF
+        last = slice(last0, F)
+        for m in range(MT):
+            add_pre(2, m, last0, last_w)
+            nc.scalar.activation(out=gate_in[:, m, last], in_=gate_in[:, m, last], func=ACT.Tanh, scale=0.5)
+        wo_quantise(0)
+        hg_il = []
+        for m in range(MT):
+            nc.vector.scalar_tensor_tensor(out=hg[:, m, last], in0=gate_in[:, m, last], scalar=1.0, in1=cand[:, m, last], op0=ALU.add, op1=ALU.mult)
+            tp = psum.tile([P, 2, P], F32, name="tp", tag="tp", bufs=2)
+            words = hg[:, m, :].bitcast(F32)
+            for u in range(2):
+                nc.tensor.transpose(tp[:, u, :], words[:, u:F // 2:2], ident[:])
+            t = keep.tile([P, P * PACK], BF16, name="hg_il%d" % m, align_bytes=64)
+            nc.scalar.copy(out=t[:].bitcast(F32).rearrange("p (r u) -> p r u", u=2), in_=tp[:].rearrange("p u r -> p r u"))
+            hg_il.append(t)
+        wo_quantise(1)
+        ys = []
+        for m in range(MT):
+            codes = keep.tile([P, P], I32, name="hg_codes%d" % m, align_bytes=64)
+            scales = keep.tile([P, P], U8, name="hg_scales%d" % m, align_bytes=64)
+            nc.vector.quantize_mx(out=codes[:].bitcast(FP8X4), scales=scales[:], in_=hg_il[m][:])
+            for half in range(2):
+                cols = slice(half * F, (half + 1) * F)
+                y_ps = psum.tile([P, F], F32, name="acc", tag="acc", bufs=6)
+                nc.tensor.matmul_mx(out=y_ps[:], lhsT=codes[:].bitcast(FP8X4), lhsT_scale=scales[:],
+                                    rhs=wo_codes[:, cols].bitcast(FP8X4), rhs_scale=wo_scales[:, cols], start=True, stop=True)
+                ys.append((m, half, y_ps))
+        for m, half, y_ps in ys:
+            y_sb = keep.tile([P, F], F32, name="y_sb%d_%d" % (m, half))
+            if half == 0:
+                nc.scalar.copy(out=y_sb[:], in_=y_ps[:])
+            else:
+                nc.vector.tensor_copy(out=y_sb[:], in_=y_ps[:])
+            nc.sync.dma_start(out=y_rows[m * P:(m + 1) * P, half * F:(half + 1) * F], in_=y_sb[:])

@@ -25,17 +25,11 @@ HT = HALO // P
 
 FLOPS = 2 * TOK * F * (TAPS * 3 * F + E)
 
-HALF = F // 2
-UNITS = [[(gate, tap, 0, F)] for gate in range(2) for tap in range(TAPS)]
-O_STRIPS = [(2, tap, half * HALF, HALF) for half in range(2) for tap in range(TAPS)]
-O_UNITS = [O_STRIPS[i:i + 2] for i in range(0, 16, 2)] + [O_STRIPS[16:17], O_STRIPS[17:18]]
-ALL_UNITS = UNITS + O_UNITS
-GROUPS = [[0], [1], [2, 3], [4, 5], [6, 7], [8, 9], [10, 11], [12, 13], [14, 15], [16, 17], [18, 19], [20, 21], [22, 23], [24, 25], [26], [27]]
-VECTOR_WIDENS = {0}
-TENSOR_INTERLEAVES = set()
-SCALAR_INTERLEAVES = {24}
-WO_ON_TENSOR = False
-LEAD = 2
+STRIPS = [(gate, tap) for gate in range(3) for tap in range(TAPS)]
+SIZES = [1,1,1,2,2,2,2,2,2,2,2,2,2,2,1,1]
+GROUPS = [STRIPS[sum(SIZES[:j]):sum(SIZES[:j + 1])] for j in range(len(SIZES))]
+VECTOR_WIDENS = [2048,0,0,768,768,768,768,768,768,768,768,768,768,768,0,0]
+TENSOR_COLUMNS = [0,0,256,256,256,256,256,256,256,256,256,256,256,256,0,0]
 
 
 def interleave_views(dst, src):
@@ -50,22 +44,14 @@ def tile_peepholeconvlstmninetap_kernel(tc, h, c, wh_bytes, wh_scale, peep_f, pe
         psum = ctx.enter_context(tc.psum_pool(name="psum", bufs=1))
         ctx.enter_context(tc.manual_schedule())
 
-        units = ALL_UNITS
-        width = [sum(s[3] for s in u) for u in units]
-        group_of = {k: gi for gi, g in enumerate(GROUPS) for k in g}
-        start_in_group = {k: sum(width[j] for j in g if j < k) for g in GROUPS for k in g}
-        group_width = [sum(width[k] for k in g) for g in GROUPS]
-
         wscale = keep.tile([P, PACK], F32, name="wscale")
         nc.sync.dma_start(out=wscale[:], in_=wh_scale.rearrange("a b (p t) o -> p (a b t o)", t=PACK))
-        wbytes = [keep.tile([P, PACK, w], U8, name="wbytes%d" % gi) for gi, w in enumerate(group_width)]
+        wbytes = [keep.tile([P, PACK, len(g) * F], U8, name="wbytes%d" % j) for j, g in enumerate(GROUPS)]
 
-        def load_w(k):
-            at = start_in_group[k]
-            for gate, tap, c0, w in units[k]:
+        def load_w(j):
+            for i, (gate, tap) in enumerate(GROUPS[j]):
                 src = wh_bytes[tap // 3, tap % 3].rearrange("(p t) n -> p t n", t=PACK)
-                nc.sync.dma_start(out=wbytes[group_of[k]][:, :, at:at + w], in_=src[:, :, gate * F + c0:gate * F + c0 + w])
-                at = at + w
+                nc.sync.dma_start(out=wbytes[j][:, :, i * F:(i + 1) * F], in_=src[:, :, gate * F:(gate + 1) * F])
 
         def load_peep(dst, src):
             rows = src.rearrange("i j f -> (i j) f")
@@ -77,33 +63,38 @@ def tile_peepholeconvlstmninetap_kernel(tc, h, c, wh_bytes, wh_scale, peep_f, pe
                     nc.sync.dma_start(out=dst[p0:p0 + n, m, :], in_=rows[r0:r0 + n, :])
                     p0 = p0 + n
 
-        load_w(0)
-        load_w(1)
         h_rows = h.rearrange("b i j f -> (b i j) f").rearrange("(m p) f -> p m f", p=P)
         h_pairs = [(m0, min(2, HT - m0)) for m0 in range(0, HT, 2)]
         h_raw = []
-        for m0, n in h_pairs:
+
+        def load_h(i):
+            m0, n = h_pairs[i]
             t = keep.tile([P, n, F], BF16, name="h_raw%d" % m0)
             nc.sync.dma_start(out=t[:], in_=h_rows[:, m0:m0 + n, :])
             h_raw.append(t)
-        for k in range(2, 6):
-            load_w(k)
-        wo_raw = keep.tile([P, PACK, E], BF16, name="wo_raw")
-        nc.sync.dma_start(out=wo_raw[:], in_=wo.rearrange("(p t) e -> p t e", t=PACK))
-        for k in range(6, 12):
-            load_w(k)
+
+        load_w(0)
+        load_w(1)
+        load_h(0)
+        load_w(2)
+        load_h(1)
+        load_h(2)
+        for j in range(3, 7):
+            load_w(j)
         c_sb = keep.tile([P, MT, F], BF16, name="c_sb")
         nc.sync.dma_start(out=c_sb[:], in_=c.rearrange("b i j f -> (b i j) f").rearrange("(m p) f -> p m f", p=P))
         pf_sb = keep.tile([P, MT, F], BF16, name="pf_sb")
         load_peep(pf_sb, peep_f)
-        for k in range(12, 20):
-            load_w(k)
+        for j in range(7, 12):
+            load_w(j)
         gain_sb = keep.tile([P, F], BF16, name="gain_sb")
         nc.sync.dma_start(out=gain_sb[:], in_=gain.partition_broadcast(P))
         po_sb = keep.tile([P, MT, F], BF16, name="po_sb")
         load_peep(po_sb, peep_o)
-        for k in range(20, len(units)):
-            load_w(k)
+        for j in range(12, len(GROUPS)):
+            load_w(j)
+        wo_raw = keep.tile([P, PACK, E], BF16, name="wo_raw")
+        nc.sync.dma_start(out=wo_raw[:], in_=wo.rearrange("(p t) e -> p t e", t=PACK))
 
         ident = keep.tile([P, P], F32, name="ident")
         make_identity(nc, ident[:])
@@ -114,58 +105,82 @@ def tile_peepholeconvlstmninetap_kernel(tc, h, c, wh_bytes, wh_scale, peep_f, pe
 
         planes = {}
 
-        def widen(gi, t):
-            if gi not in planes:
-                planes[gi] = work.tile([P, PACK, group_width[gi]], BF16, name="planes", tag="planes", bufs=4)
-            src = wbytes[gi][:, t, :].bitcast(FP8)
-            if GROUPS[gi][0] in VECTOR_WIDENS:
-                nc.vector.tensor_scalar(out=planes[gi][:, t, :], in0=src, scalar1=wscale[:, t:t + 1], scalar2=None, op0=ALU.mult)
-            else:
-                nc.scalar.activation(out=planes[gi][:, t, :], in_=src, func=ACT.Copy, scale=wscale[:, t:t + 1])
-
-        widen_at = {}
-        for gi, g in enumerate(GROUPS):
-            for t in range(PACK):
-                widen_at.setdefault(max(-1, g[0] - LEAD - len(g) + 1 + t * len(g) // PACK), []).append((gi, t))
         il = {}
+        banks = {}
         acc = {}
 
-        def tensor_interleave(dst, src, n):
+        def plane_tile(j):
+            if j not in planes:
+                planes[j] = work.tile([P, PACK, len(GROUPS[j]) * F], BF16, name="planes", tag="planes", bufs=4)
+            return planes[j]
+
+        def vector_columns(j, t):
+            n = len(GROUPS[j]) * F
+            return min(n, max(0, VECTOR_WIDENS[j] - (PACK - 1 - t) * n))
+
+        def widen_vector(j):
+            for t in range(PACK):
+                x = vector_columns(j, t)
+                if x > 0:
+                    nc.vector.tensor_scalar(out=plane_tile(j)[:, t, 0:x], in0=wbytes[j][:, t, 0:x].bitcast(FP8),
+                                            scalar1=wscale[:, t:t + 1], scalar2=None, op0=ALU.mult)
+
+        def widen_scalar(j, ts):
+            n = len(GROUPS[j]) * F
+            for t in ts:
+                x = vector_columns(j, t)
+                if x < n:
+                    nc.scalar.activation(out=plane_tile(j)[:, t, x:n], in_=wbytes[j][:, t, x:n].bitcast(FP8), func=ACT.Copy,
+                                         scale=wscale[:, t:t + 1])
+
+        def tensor_interleave(src, n):
+            tps = []
             for b0 in range(0, n, 2 * P):
-                tp = psum.tile([P, 2 * F], BF16, name="tp", tag="tp", bufs=2)
-                for j in range(2):
-                    nc.tensor.matmul(out=tp[:, j * F:(j + 1) * F], lhsT=ident_b[:],
-                                     rhs=src[:, :, b0 + j * P:b0 + (j + 1) * P].rearrange("p t n -> p n t"), start=True, stop=True)
-                nc.scalar.copy(out=dst[:, b0 * PACK:(b0 + 2 * P) * PACK], in_=tp[:])
+                w = min(2 * P, n - b0)
+                tp = psum.tile([P, w * PACK], BF16, name="tp", tag="tp", bufs=2)
+                for i in range(0, w, P):
+                    nc.tensor.matmul(out=tp[:, i * PACK:(i + P) * PACK], lhsT=ident_b[:],
+                                     rhs=src[:, :, b0 + i:b0 + i + P].rearrange("p t n -> p n t"), start=True, stop=True)
+                tps.append((b0, w, tp))
+            return tps
 
-        def interleave(k):
-            at = start_in_group[k]
-            il[k] = work.tile([P, width[k], PACK], BF16, name="il", tag="il", bufs=4, align_bytes=64)
-            src = planes[group_of[k]][:, :, at:at + width[k]]
-            if k in TENSOR_INTERLEAVES:
-                tensor_interleave(il[k][:].rearrange("p n t -> p (n t)"), src, width[k])
-                return
-            dst, src = interleave_views(il[k][:], src)
-            if k in SCALAR_INTERLEAVES:
-                nc.scalar.copy(out=dst, in_=src)
-            else:
-                nc.vector.tensor_copy(out=dst, in_=src)
+        def empty_banks(dst, tps):
+            for b0, w, tp in tps:
+                nc.scalar.copy(out=dst[:, b0:b0 + w, :].rearrange("p n t -> p (n t)"), in_=tp[:])
 
-        for gi, t in widen_at[-1]:
-            widen(gi, t)
-        interleave(0)
+        def il_tile(j):
+            if j not in il:
+                il[j] = work.tile([P, len(GROUPS[j]) * F, PACK], BF16, name="il", tag="il", bufs=3, align_bytes=64)
+            return il[j]
+
+        def interleave_tensor(j):
+            n = len(GROUPS[j]) * F
+            banks[j] = tensor_interleave(planes[j][:, :, n - TENSOR_COLUMNS[j]:n], TENSOR_COLUMNS[j])
+
+        def interleave_scalar(j):
+            n = len(GROUPS[j]) * F
+            empty_banks(il_tile(j)[:, n - TENSOR_COLUMNS[j]:n, :], banks[j])
+
+        def interleave_vector(j):
+            n = len(GROUPS[j]) * F - TENSOR_COLUMNS[j]
+            dst, src = interleave_views(il_tile(j)[:, 0:n, :], planes[j][:, :, 0:n])
+            nc.vector.tensor_copy(out=dst, in_=src)
+
 
         h_il = keep.tile([P, HALO * PACK], BF16, name="h_il", align_bytes=64)
         h_codes = keep.tile([P, HALO], I32, name="h_codes", align_bytes=64)
-        for (m0, n), raw in zip(h_pairs, h_raw):
+
+        def turn_h(i):
+            m0, n = h_pairs[i]
             tp = psum.tile([P, 2, 2, P], F32, name="tp", tag="tp", bufs=2)
             for m in range(n):
-                words = raw[:, m, :].bitcast(F32)
+                words = h_raw[i][:, m, :].bitcast(F32)
                 for u in range(2):
                     nc.tensor.transpose(tp[:, m, u, :], words[:, u:F // 2:2], ident[:])
             dst = h_il[:, m0 * P * PACK:(m0 + n) * P * PACK].bitcast(F32).rearrange("p (m r u) -> p m r u", m=n, u=2)
             nc.vector.tensor_copy(out=dst, in_=tp[:, 0:n, :, :].rearrange("p m u r -> p m r u"))
-        for c0, c1 in ((0, 512), (512, HALO)):
+
+        def quantise_h(c0, c1):
             nc.vector.quantize_mx(out=h_codes[:, c0:c1].bitcast(FP8X4), scales=h_scales[:, c0:c1],
                                   in_=h_il[:, c0 * PACK:c1 * PACK])
 
@@ -190,32 +205,42 @@ def tile_peepholeconvlstmninetap_kernel(tc, h, c, wh_bytes, wh_scale, peep_f, pe
             nc.vector.tensor_copy(out=win_codes[:, tap, :].rearrange("p (b i j) -> p b i j", i=YY, j=XX),
                                   in_=src[:, :, dy:dy + YY, dx:dx + XX])
 
-        def quantise_multiply(k):
-            codes = work.tile([P, width[k]], I32, name="codes", tag="codes", bufs=4, align_bytes=64)
-            scales = work.tile([P, width[k]], U8, name="scales", tag="scales", bufs=4, align_bytes=64)
-            nc.vector.quantize_mx(out=codes[:].bitcast(FP8X4), scales=scales[:], in_=il[k][:].rearrange("p n t -> p (n t)"))
-            at = 0
-            for gate, tap, c0, w in units[k]:
-                for m in range(MT):
-                    if tap == 0:
-                        acc[gate, m, c0] = psum.tile([P, w], F32, name="acc", tag="acc", bufs=6)
-                    nc.tensor.matmul_mx(out=acc[gate, m, c0][:], lhsT=win_codes[:, tap, m * P:(m + 1) * P].bitcast(FP8X4),
-                                        lhsT_scale=win_scales[:, tap, m * P:(m + 1) * P],
-                                        rhs=codes[:, at:at + w].bitcast(FP8X4), rhs_scale=scales[:, at:at + w],
-                                        start=(tap == 0), stop=(tap == TAPS - 1))
-                at = at + w
+        quantised = {}
+
+        def quantise(j, i):
+            codes = work.tile([P, F], I32, name="codes", tag="codes", bufs=6, align_bytes=64)
+            scales = work.tile([P, F], U8, name="scales", tag="scales", bufs=6, align_bytes=64)
+            nc.vector.quantize_mx(out=codes[:].bitcast(FP8X4), scales=scales[:],
+                                  in_=il[j][:, i * F:(i + 1) * F, :].rearrange("p n t -> p (n t)"))
+            quantised[j, i] = (codes, scales)
+
+        def multiply(j):
+            for i in range(len(GROUPS[j])):
+                if GROUPS[j][i][1] < TAPS - 1:
+                    multiply_strip(j, i)
+
+        def multiply_strip(j, i):
+            gate, tap = GROUPS[j][i]
+            codes, scales = quantised[j, i]
+            for m in range(MT):
+                if tap == 0:
+                    acc[gate, m] = psum.tile([P, F], F32, name="acc", tag="acc", bufs=6)
+                nc.tensor.matmul_mx(out=acc[gate, m][:], lhsT=win_codes[:, tap, m * P:(m + 1) * P].bitcast(FP8X4),
+                                    lhsT_scale=win_scales[:, tap, m * P:(m + 1) * P],
+                                    rhs=codes[:].bitcast(FP8X4), rhs_scale=scales[:],
+                                    start=(tap == 0), stop=(tap == TAPS - 1))
 
         wo_il = keep.tile([P, E, PACK], BF16, name="wo_il", align_bytes=64)
         wo_codes = keep.tile([P, E], I32, name="wo_codes", align_bytes=64)
         wo_scales = keep.tile([P, E], U8, name="wo_scales", align_bytes=64)
 
-        def wo_interleave(half):
-            cols = slice(half * F, (half + 1) * F)
-            if WO_ON_TENSOR:
-                tensor_interleave(wo_il[:, cols, :].rearrange("p n t -> p (n t)"), wo_raw[:, :, cols], F)
-                return
-            dst, src = interleave_views(wo_il[:, cols, :], wo_raw[:, :, cols])
-            nc.scalar.copy(out=dst, in_=src)
+        wo_banks = {}
+
+        def wo_tensor(half):
+            wo_banks[half] = tensor_interleave(wo_raw[:, :, half * F:(half + 1) * F], F)
+
+        def wo_scalar(half):
+            empty_banks(wo_il[:, half * F:(half + 1) * F, :], wo_banks[half])
 
         def wo_quantise(half):
             cols = slice(half * F, (half + 1) * F)
@@ -237,8 +262,8 @@ def tile_peepholeconvlstmninetap_kernel(tc, h, c, wh_bytes, wh_scale, peep_f, pe
         def halve_c():
             nc.vector.tensor_scalar(out=flat(c_half), in0=flat(c_sb), scalar1=0.5, scalar2=None, op0=ALU.mult)
 
-        def add_pre(gate, m, c0, w):
-            nc.vector.tensor_tensor(out=gate_in[:, m, c0:c0 + w], in0=acc[gate, m, c0][:], in1=gate_in[:, m, c0:c0 + w], op=ALU.add)
+        def add_pre(gate, m):
+            nc.vector.tensor_tensor(out=gate_in[:, m, :], in0=acc[gate, m][:], in1=gate_in[:, m, :], op=ALU.add)
 
         def tanh_f():
             nc.scalar.activation(out=flat(gate_in), in_=flat(gate_in), func=ACT.Tanh, scale=0.5)
@@ -246,97 +271,150 @@ def tile_peepholeconvlstmninetap_kernel(tc, h, c, wh_bytes, wh_scale, peep_f, pe
         def keep_term():
             nc.vector.scalar_tensor_tensor(out=flat(kept), in0=flat(gate_in), scalar=1.0, in1=flat(c_half), op0=ALU.add, op1=ALU.mult)
 
-        def tanh_g():
-            for m in range(MT):
-                nc.scalar.activation(out=cand[:, m, :], in_=acc[1, m, 0][:], func=ACT.Tanh)
+        def tanh_g(m):
+            nc.scalar.activation(out=cand[:, m, :], in_=acc[1, m][:], func=ACT.Tanh)
 
-        def cand_term():
-            nc.vector.scalar_tensor_tensor(out=flat(cand), in0=flat(gate_in), scalar=-1.0, in1=flat(cand), op0=ALU.add, op1=ALU.mult)
+        c_rows = out_1.rearrange("b i j f -> (b i j) f")
 
-        def cell():
-            nc.vector.scalar_tensor_tensor(out=flat(c_new), in0=flat(cand), scalar=-0.5, in1=flat(kept), op0=ALU.mult, op1=ALU.add)
-            nc.sync.dma_start(out=out_1.rearrange("b i j f -> (b i j) f").rearrange("(m p) f -> p m f", p=P), in_=c_new[:])
+        def cand_term(m):
+            nc.vector.scalar_tensor_tensor(out=cand[:, m, :], in0=gate_in[:, m, :], scalar=-1.0, in1=cand[:, m, :], op0=ALU.add, op1=ALU.mult)
 
-        def peep_o_term():
-            nc.vector.tensor_tensor(out=flat(gate_in), in0=flat(c_new), in1=flat(po_sb), op=ALU.mult)
+        def cell(m):
+            nc.vector.scalar_tensor_tensor(out=c_new[:, m, :], in0=cand[:, m, :], scalar=-0.5, in1=kept[:, m, :], op0=ALU.mult, op1=ALU.add)
+            nc.sync.dma_start(out=c_rows[m * P:(m + 1) * P, :], in_=c_new[:, m, :])
 
-        def tanh_c():
-            nc.scalar.activation(out=flat(cand), in_=flat(c_new), func=ACT.Tanh)
+        def peep_o_term(m):
+            nc.vector.tensor_tensor(out=gate_in[:, m, :], in0=c_new[:, m, :], in1=po_sb[:, m, :], op=ALU.mult)
 
-        def gain_term():
-            for m in range(MT):
-                nc.vector.scalar_tensor_tensor(out=cand[:, m, :], in0=cand[:, m, :], scalar=0.5, in1=gain_sb[:], op0=ALU.mult, op1=ALU.mult)
+        def tanh_c(m):
+            nc.scalar.activation(out=cand[:, m, :], in_=c_new[:, m, :], func=ACT.Tanh)
+
+        def gain_term(m):
+            nc.vector.scalar_tensor_tensor(out=cand[:, m, :], in0=cand[:, m, :], scalar=0.5, in1=gain_sb[:], op0=ALU.mult, op1=ALU.mult)
 
         def add_f():
             for m in range(MT):
-                add_pre(0, m, 0, F)
-
-        hg = keep.tile([P, MT, F], BF16, name="hg")
-
-        def add_o_first():
-            for m in range(MT):
-                add_pre(2, m, 0, HALF)
-
-        def tanh_o_first():
-            nc.scalar.activation(out=gate_in[:, :, 0:HALF], in_=gate_in[:, :, 0:HALF], func=ACT.Tanh, scale=0.5)
-
-        def hg_first():
-            nc.vector.scalar_tensor_tensor(out=hg[:, :, 0:HALF], in0=gate_in[:, :, 0:HALF], scalar=1.0, in1=cand[:, :, 0:HALF], op0=ALU.add, op1=ALU.mult)
-
-        after_il = {0: [shift_scales, lambda: window_codes(0), lambda: window_scales(0)], 3: [lambda: window_scales(1)], 6: [lambda: window_scales(2)],
-            7: [peep_f_term], 8: [halve_c], 11: [add_f], 14: [keep_term], 20: [cand_term], 21: [cell], 22: [peep_o_term], 23: [gain_term], 25: [add_o_first], 27: [hg_first]}
-        after_q = {12: [tanh_f], 18: [tanh_g], 21: [tanh_c], 25: [tanh_o_first], 26: [lambda: wo_interleave(0), lambda: wo_interleave(1)]}
-        for k in range(len(units)):
-            for gi, t in widen_at.get(k, []):
-                widen(gi, t)
-            early = TENSOR_INTERLEAVES | SCALAR_INTERLEAVES
-            if k + 1 in early:
-                interleave(k + 1)
-            if k >= 1 and k not in early:
-                interleave(k)
-            if 1 <= k < TAPS:
-                window_codes(k)
-            for step in after_il.get(k, []):
-                step()
-            if k >= 1:
-                quantise_multiply(k - 1)
-            for step in after_q.get(k, []):
-                step()
-        quantise_multiply(len(units) - 1)
+                add_pre(0, m)
 
         y_rows = out_0.rearrange("b i j e -> (b i j) e")
-        last0, last_w = HALF, HALF
-        last = slice(last0, F)
-        for m in range(MT):
-            add_pre(2, m, last0, last_w)
-            nc.scalar.activation(out=gate_in[:, m, last], in_=gate_in[:, m, last], func=ACT.Tanh, scale=0.5)
-        wo_quantise(0)
-        hg_il = []
-        for m in range(MT):
-            nc.vector.scalar_tensor_tensor(out=hg[:, m, last], in0=gate_in[:, m, last], scalar=1.0, in1=cand[:, m, last], op0=ALU.add, op1=ALU.mult)
+        hg = keep.tile([P, MT, F], BF16, name="hg")
+        hg_il = {}
+        y_ps = {}
+
+        def gate_o(m):
+            add_pre(2, m)
+            nc.scalar.activation(out=gate_in[:, m, :], in_=gate_in[:, m, :], func=ACT.Tanh, scale=0.5)
+
+        def hidden(m):
+            nc.vector.scalar_tensor_tensor(out=hg[:, m, :], in0=gate_in[:, m, :], scalar=1.0, in1=cand[:, m, :], op0=ALU.add, op1=ALU.mult)
             tp = psum.tile([P, 2, P], F32, name="tp", tag="tp", bufs=2)
             words = hg[:, m, :].bitcast(F32)
             for u in range(2):
                 nc.tensor.transpose(tp[:, u, :], words[:, u:F // 2:2], ident[:])
-            t = keep.tile([P, P * PACK], BF16, name="hg_il%d" % m, align_bytes=64)
-            nc.scalar.copy(out=t[:].bitcast(F32).rearrange("p (r u) -> p r u", u=2), in_=tp[:].rearrange("p u r -> p r u"))
-            hg_il.append(t)
-        wo_quantise(1)
-        ys = []
-        for m in range(MT):
+            hg_il[m] = keep.tile([P, P * PACK], BF16, name="hg_il%d" % m, align_bytes=64)
+            nc.scalar.copy(out=hg_il[m][:].bitcast(F32).rearrange("p (r u) -> p r u", u=2), in_=tp[:].rearrange("p u r -> p r u"))
+
+        hg_q = {}
+
+        def hidden_quantise(m):
             codes = keep.tile([P, P], I32, name="hg_codes%d" % m, align_bytes=64)
             scales = keep.tile([P, P], U8, name="hg_scales%d" % m, align_bytes=64)
             nc.vector.quantize_mx(out=codes[:].bitcast(FP8X4), scales=scales[:], in_=hg_il[m][:])
-            for half in range(2):
-                cols = slice(half * F, (half + 1) * F)
-                y_ps = psum.tile([P, F], F32, name="acc", tag="acc", bufs=6)
-                nc.tensor.matmul_mx(out=y_ps[:], lhsT=codes[:].bitcast(FP8X4), lhsT_scale=scales[:],
-                                    rhs=wo_codes[:, cols].bitcast(FP8X4), rhs_scale=wo_scales[:, cols], start=True, stop=True)
-                ys.append((m, half, y_ps))
-        for m, half, y_ps in ys:
+            hg_q[m] = (codes, scales)
+
+        def project(m, half):
+            codes, scales = hg_q[m]
+            cols = slice(half * F, (half + 1) * F)
+            y_ps[m, half] = psum.tile([P, F], F32, name="acc", tag="acc", bufs=6)
+            nc.tensor.matmul_mx(out=y_ps[m, half][:], lhsT=codes[:].bitcast(FP8X4), lhsT_scale=scales[:],
+                                rhs=wo_codes[:, cols].bitcast(FP8X4), rhs_scale=wo_scales[:, cols], start=True, stop=True)
+
+        def store(m, half, on_scalar):
             y_sb = keep.tile([P, F], F32, name="y_sb%d_%d" % (m, half))
-            if half == 0:
-                nc.scalar.copy(out=y_sb[:], in_=y_ps[:])
+            if on_scalar:
+                nc.scalar.copy(out=y_sb[:], in_=y_ps[m, half][:])
             else:
-                nc.vector.tensor_copy(out=y_sb[:], in_=y_ps[:])
+                nc.vector.tensor_copy(out=y_sb[:], in_=y_ps[m, half][:])
             nc.sync.dma_start(out=y_rows[m * P:(m + 1) * P, half * F:(half + 1) * F], in_=y_sb[:])
+
+        vector_steps = {5: [peep_f_term], 6: [halve_c], 7: [add_f], 9: [keep_term], 12: [lambda: cell(0), lambda: cell(1)], 13: [lambda: gain_term(0)], 14: [lambda: gain_term(1), lambda: peep_o_term(1)], 15: [lambda: gain_term(2), lambda: peep_o_term(2)]}
+        scalar_steps = {8: [tanh_f], 11: [lambda: tanh_g(0), lambda: tanh_g(1), lambda: tanh_g(2)], 13: [lambda: tanh_c(0), lambda: tanh_c(1), lambda: tanh_c(2)]}
+        late_steps = {13: [lambda: wo_tensor(0)], 14: [lambda: wo_scalar(0)]}
+        after_steps = {11: [lambda: cand_term(0), lambda: cand_term(1), lambda: cand_term(2)], 14: [lambda: multiply(14), lambda: wo_tensor(1), lambda: wo_scalar(1), lambda: early.add(14)]}
+        middle_steps = {12: [lambda: cell(2)], 13: [lambda: peep_o_term(0)]}
+        early = set()
+        last = len(GROUPS) - 1
+        widen_vector(0)
+        widen_scalar(1, range(PACK))
+        interleave_vector(0)
+        turn_h(0)
+        quantise(0, 0)
+        turn_h(1)
+        turn_h(2)
+        quantise_h(0, F)
+        quantise_h(F, HALO)
+        interleave_vector(1)
+        shift_scales()
+        window_codes(0)
+        window_scales(0)
+        for j in range(1, len(GROUPS)):
+            if j < last:
+                widen_scalar(j + 1, range(0, 2))
+            if j > 1:
+                interleave_scalar(j)
+            for step in scalar_steps.get(j, []):
+                step()
+            if j < last:
+                widen_scalar(j + 1, range(2, PACK))
+            if j > 1:
+                interleave_vector(j)
+            if j + 2 <= last:
+                widen_vector(j + 2)
+            for gate, tap in GROUPS[j]:
+                if gate == 0:
+                    window_codes(tap)
+                    if tap % 3 == 0:
+                        window_scales(tap // 3)
+            for step in vector_steps.get(j, []):
+                step()
+            if j < last:
+                interleave_tensor(j + 1)
+            for step in late_steps.get(j, []):
+                step()
+            if j - 1 not in early:
+                multiply(j - 1)
+            for i in range(len(GROUPS[j])):
+                quantise(j, i)
+                if GROUPS[j][i][1] == TAPS - 1:
+                    if i > 0:
+                        multiply(j)
+                        early.add(j)
+                    multiply_strip(j, i)
+                if i == 0:
+                    for step in middle_steps.get(j, []):
+                        step()
+            for step in after_steps.get(j, []):
+                step()
+        wo_quantise(0)
+        gate_o(0)
+        gate_o(1)
+        gate_o(2)
+        hidden(0)
+        hidden(1)
+        hidden(2)
+        hidden_quantise(0)
+        project(0, 0)
+        wo_quantise(1)
+        project(0, 1)
+        hidden_quantise(1)
+        project(1, 0)
+        project(1, 1)
+        store(0, 0, True)
+        hidden_quantise(2)
+        project(2, 0)
+        project(2, 1)
+        store(0, 1, False)
+        store(1, 0, True)
+        store(1, 1, False)
+        store(2, 0, True)
+        store(2, 1, False)

@@ -13,47 +13,77 @@ ACT = mybir.ActivationFunctionType
 ALU = mybir.AluOpType
 
 B, YY, XX, F, E = 8, 6, 8, 512, 1024
-YP, XP = YY + 2, XX + 2
+SIDE = 3
+TAPS = SIDE * SIDE
+YP, XP = YY + SIDE - 1, XX + SIDE - 1
 P = 128
 PACK = 4
-TAPS = 9
 POS = YY * XX
 TOK = B * POS
 MT = TOK // P
 HALO = B * YP * XP
 HT = HALO // P
+GATE_F, GATE_G, GATE_O = 0, 1, 2
+BANK_COLUMNS = 256
 
 FLOPS = 2 * TOK * F * (TAPS * 3 * F + E)
 
-STRIPS = [(gate, tap) for gate in range(3) for tap in range(TAPS)]
-SIZES = [1,1,1,2,2,2,2,2,2,2,2,2,2,2,1,1]
-GROUPS = [STRIPS[sum(SIZES[:j]):sum(SIZES[:j + 1])] for j in range(len(SIZES))]
-VECTOR_WIDENS = [2048,0,0,768,768,768,768,768,768,768,768,768,768,768,0,0]
-TENSOR_COLUMNS = [0,0,256,256,256,256,256,256,256,256,256,256,256,256,0,0]
+STRIPS = [(gate, tap) for gate in (GATE_F, GATE_G, GATE_O) for tap in range(TAPS)]
+SINGLES_FIRST, SINGLES_LAST = 3, 2
+GROUPS = (
+    [STRIPS[s:s + 1] for s in range(SINGLES_FIRST)]
+    + [STRIPS[s:s + 2] for s in range(SINGLES_FIRST, len(STRIPS) - SINGLES_LAST, 2)]
+    + [STRIPS[s:s + 1] for s in range(len(STRIPS) - SINGLES_LAST, len(STRIPS))]
+)
+LAST = len(GROUPS) - 1
+F_END = [j for j, g in enumerate(GROUPS) if (GATE_F, TAPS - 1) in g][0]
+G_END = [j for j, g in enumerate(GROUPS) if (GATE_G, TAPS - 1) in g][0]
+
+VECTOR_SHARE = 896
+VECTOR_SHARE_LATE = 2 * F
+PROMPT_FROM = 4
+PLANE_BUFS, INTERLEAVED_BUFS, CODE_BUFS = 4, 3, 6
+SUM_BANKS, TURN_BANKS = 2 * MT, 2
+
+
+def group_columns(j):
+    return len(GROUPS[j]) * F
+
+
+def vector_widens(j, t):
+    if j == 0:
+        return F
+    if len(GROUPS[j]) == 1 or t < PACK - 1:
+        return 0
+    return VECTOR_SHARE if j <= G_END else VECTOR_SHARE_LATE
+
+
+def tensor_columns(j):
+    return BANK_COLUMNS if 2 <= j <= LAST - SINGLES_LAST else 0
 
 
 def interleave_views(dst, src):
-    return (dst.rearrange("p (c i) t -> p c t i", i=4), src.rearrange("p t (c i) -> p c t i", i=4))
+    return dst.rearrange("p (c i) t -> p c t i", i=4), src.rearrange("p t (c i) -> p c t i", i=4)
 
 
 def tile_peepholeconvlstmninetap_kernel(tc, h, c, wh_bytes, wh_scale, peep_f, peep_o, gain, wo, out_0, out_1):
     nc = tc.nc
     with ExitStack() as ctx:
         keep = ctx.enter_context(tc.tile_pool(name="keep", bufs=1))
-        work = ctx.enter_context(tc.tile_pool(name="work", bufs=3))
+        work = ctx.enter_context(tc.tile_pool(name="work", bufs=INTERLEAVED_BUFS))
         psum = ctx.enter_context(tc.psum_pool(name="psum", bufs=1))
         ctx.enter_context(tc.manual_schedule())
 
         wscale = keep.tile([P, PACK], F32, name="wscale")
         nc.sync.dma_start(out=wscale[:], in_=wh_scale.rearrange("a b (p t) o -> p (a b t o)", t=PACK))
-        wbytes = [keep.tile([P, PACK, len(g) * F], U8, name="wbytes%d" % j) for j, g in enumerate(GROUPS)]
+        wbytes = [keep.tile([P, PACK, group_columns(j)], U8, name="wbytes%d" % j) for j in range(len(GROUPS))]
 
-        def load_w(j):
+        def load_w(j, t0=0, t1=PACK):
             for i, (gate, tap) in enumerate(GROUPS[j]):
-                src = wh_bytes[tap // 3, tap % 3].rearrange("(p t) n -> p t n", t=PACK)
-                nc.sync.dma_start(out=wbytes[j][:, :, i * F:(i + 1) * F], in_=src[:, :, gate * F:(gate + 1) * F])
+                src = wh_bytes[tap // SIDE, tap % SIDE].rearrange("(p t) n -> p t n", t=PACK)
+                nc.sync.dma_start(out=wbytes[j][:, t0:t1, i * F:(i + 1) * F], in_=src[:, t0:t1, gate * F:(gate + 1) * F])
 
-        def load_peep(dst, src):
+        def load_peephole(dst, src):
             rows = src.rearrange("i j f -> (i j) f")
             for m in range(MT):
                 p0 = 0
@@ -64,357 +94,332 @@ def tile_peepholeconvlstmninetap_kernel(tc, h, c, wh_bytes, wh_scale, peep_f, pe
                     p0 = p0 + n
 
         h_rows = h.rearrange("b i j f -> (b i j) f").rearrange("(m p) f -> p m f", p=P)
-        h_pairs = [(m0, min(2, HT - m0)) for m0 in range(0, HT, 2)]
-        h_raw = []
+        h_pieces = [(m0, min(2, HT - m0)) for m0 in range(0, HT, 2)]
+        h_raw = [keep.tile([P, n, F], BF16, name="h_raw%d" % m0) for m0, n in h_pieces]
 
         def load_h(i):
-            m0, n = h_pairs[i]
-            t = keep.tile([P, n, F], BF16, name="h_raw%d" % m0)
-            nc.sync.dma_start(out=t[:], in_=h_rows[:, m0:m0 + n, :])
-            h_raw.append(t)
+            m0, n = h_pieces[i]
+            nc.sync.dma_start(out=h_raw[i][:], in_=h_rows[:, m0:m0 + n, :])
 
-        load_w(0)
-        load_w(1)
+        for t0 in (0, PACK // 2):
+            load_w(1, t0, t0 + PACK // 2)
+            load_w(0, t0, t0 + PACK // 2)
         load_h(0)
         load_w(2)
         load_h(1)
         load_h(2)
-        for j in range(3, 7):
+        for j in range(SINGLES_FIRST, F_END + 2):
             load_w(j)
         c_sb = keep.tile([P, MT, F], BF16, name="c_sb")
         nc.sync.dma_start(out=c_sb[:], in_=c.rearrange("b i j f -> (b i j) f").rearrange("(m p) f -> p m f", p=P))
-        pf_sb = keep.tile([P, MT, F], BF16, name="pf_sb")
-        load_peep(pf_sb, peep_f)
-        for j in range(7, 12):
+        peep_f_sb = keep.tile([P, MT, F], BF16, name="peep_f_sb")
+        load_peephole(peep_f_sb, peep_f)
+        for j in range(F_END + 2, G_END + 2):
             load_w(j)
         gain_sb = keep.tile([P, F], BF16, name="gain_sb")
         nc.sync.dma_start(out=gain_sb[:], in_=gain.partition_broadcast(P))
-        po_sb = keep.tile([P, MT, F], BF16, name="po_sb")
-        load_peep(po_sb, peep_o)
-        for j in range(12, len(GROUPS)):
+        peep_o_sb = keep.tile([P, MT, F], BF16, name="peep_o_sb")
+        load_peephole(peep_o_sb, peep_o)
+        for j in range(G_END + 2, len(GROUPS)):
             load_w(j)
-        wo_raw = keep.tile([P, PACK, E], BF16, name="wo_raw")
-        nc.sync.dma_start(out=wo_raw[:], in_=wo.rearrange("(p t) e -> p t e", t=PACK))
+        wo_planes = keep.tile([P, PACK, E], BF16, name="wo_planes")
+        nc.sync.dma_start(out=wo_planes[:], in_=wo.rearrange("(p t) e -> p t e", t=PACK))
 
-        ident = keep.tile([P, P], F32, name="ident")
-        make_identity(nc, ident[:])
-        ident_b = keep.tile([P, P], BF16, name="ident_b")
-        make_identity(nc, ident_b[:])
+        ident_f32 = keep.tile([P, P], F32, name="ident_f32")
+        make_identity(nc, ident_f32[:])
+        ident_bf16 = keep.tile([P, P], BF16, name="ident_bf16")
+        make_identity(nc, ident_bf16[:])
         h_scales = keep.tile([P, HALO], U8, name="h_scales", align_bytes=64)
         nc.vector.memset(h_scales[:].bitcast(I32), 0)
 
-        planes = {}
-
-        il = {}
-        banks = {}
-        acc = {}
+        planes, interleaved, banks, quantised, sums = {}, {}, {}, {}, {}
 
         def plane_tile(j):
             if j not in planes:
-                planes[j] = work.tile([P, PACK, len(GROUPS[j]) * F], BF16, name="planes", tag="planes", bufs=4)
+                planes[j] = work.tile([P, PACK, group_columns(j)], BF16, name="planes", tag="planes", bufs=PLANE_BUFS)
             return planes[j]
 
-        def vector_columns(j, t):
-            n = len(GROUPS[j]) * F
-            return min(n, max(0, VECTOR_WIDENS[j] - (PACK - 1 - t) * n))
+        def interleaved_tile(j):
+            if j not in interleaved:
+                interleaved[j] = work.tile([P, group_columns(j), PACK], BF16, name="interleaved", tag="interleaved",
+                                           bufs=INTERLEAVED_BUFS, align_bytes=64)
+            return interleaved[j]
 
-        def widen_vector(j):
+        def widen_on_vector(j):
             for t in range(PACK):
-                x = vector_columns(j, t)
+                x = vector_widens(j, t)
                 if x > 0:
                     nc.vector.tensor_scalar(out=plane_tile(j)[:, t, 0:x], in0=wbytes[j][:, t, 0:x].bitcast(FP8),
                                             scalar1=wscale[:, t:t + 1], scalar2=None, op0=ALU.mult)
 
-        def widen_scalar(j, ts):
-            n = len(GROUPS[j]) * F
+        def widen_on_scalar(j, ts):
+            n = group_columns(j)
             for t in ts:
-                x = vector_columns(j, t)
+                x = vector_widens(j, t)
                 if x < n:
-                    nc.scalar.activation(out=plane_tile(j)[:, t, x:n], in_=wbytes[j][:, t, x:n].bitcast(FP8), func=ACT.Copy,
-                                         scale=wscale[:, t:t + 1])
+                    nc.scalar.activation(out=plane_tile(j)[:, t, x:n], in_=wbytes[j][:, t, x:n].bitcast(FP8),
+                                         func=ACT.Copy, scale=wscale[:, t:t + 1])
 
-        def tensor_interleave(src, n):
-            tps = []
-            for b0 in range(0, n, 2 * P):
-                w = min(2 * P, n - b0)
-                tp = psum.tile([P, w * PACK], BF16, name="tp", tag="tp", bufs=2)
-                for i in range(0, w, P):
-                    nc.tensor.matmul(out=tp[:, i * PACK:(i + P) * PACK], lhsT=ident_b[:],
-                                     rhs=src[:, :, b0 + i:b0 + i + P].rearrange("p t n -> p n t"), start=True, stop=True)
-                tps.append((b0, w, tp))
-            return tps
+        def interleave_into_bank(src, tag, bufs):
+            bank = psum.tile([P, BANK_COLUMNS * PACK], BF16, name=tag, tag=tag, bufs=bufs)
+            for c0 in range(0, BANK_COLUMNS, P):
+                nc.tensor.matmul(out=bank[:, c0 * PACK:(c0 + P) * PACK], lhsT=ident_bf16[:],
+                                 rhs=src[:, :, c0:c0 + P].rearrange("p t n -> p n t"), start=True, stop=True)
+            return bank
 
-        def empty_banks(dst, tps):
-            for b0, w, tp in tps:
-                nc.scalar.copy(out=dst[:, b0:b0 + w, :].rearrange("p n t -> p (n t)"), in_=tp[:])
+        def empty_bank(dst, bank):
+            nc.scalar.copy(out=dst.rearrange("p n t -> p (n t)"), in_=bank[:])
 
-        def il_tile(j):
-            if j not in il:
-                il[j] = work.tile([P, len(GROUPS[j]) * F, PACK], BF16, name="il", tag="il", bufs=3, align_bytes=64)
-            return il[j]
+        def interleave_by_copy(j):
+            n = group_columns(j) - tensor_columns(j)
+            dst, src = interleave_views(interleaved_tile(j)[:, 0:n, :], planes[j][:, :, 0:n])
+            if j == LAST:
+                nc.scalar.copy(out=dst, in_=src)
+            else:
+                nc.vector.tensor_copy(out=dst, in_=src)
 
-        def interleave_tensor(j):
-            n = len(GROUPS[j]) * F
-            banks[j] = tensor_interleave(planes[j][:, :, n - TENSOR_COLUMNS[j]:n], TENSOR_COLUMNS[j])
-
-        def interleave_scalar(j):
-            n = len(GROUPS[j]) * F
-            empty_banks(il_tile(j)[:, n - TENSOR_COLUMNS[j]:n, :], banks[j])
-
-        def interleave_vector(j):
-            n = len(GROUPS[j]) * F - TENSOR_COLUMNS[j]
-            dst, src = interleave_views(il_tile(j)[:, 0:n, :], planes[j][:, :, 0:n])
-            nc.vector.tensor_copy(out=dst, in_=src)
-
-
-        h_il = keep.tile([P, HALO * PACK], BF16, name="h_il", align_bytes=64)
-        h_codes = keep.tile([P, HALO], I32, name="h_codes", align_bytes=64)
-
-        def turn_h(i):
-            m0, n = h_pairs[i]
-            tp = psum.tile([P, 2, 2, P], F32, name="tp", tag="tp", bufs=2)
-            for m in range(n):
-                words = h_raw[i][:, m, :].bitcast(F32)
-                for u in range(2):
-                    nc.tensor.transpose(tp[:, m, u, :], words[:, u:F // 2:2], ident[:])
-            dst = h_il[:, m0 * P * PACK:(m0 + n) * P * PACK].bitcast(F32).rearrange("p (m r u) -> p m r u", m=n, u=2)
-            nc.vector.tensor_copy(out=dst, in_=tp[:, 0:n, :, :].rearrange("p m u r -> p m r u"))
-
-        def quantise_h(c0, c1):
-            nc.vector.quantize_mx(out=h_codes[:, c0:c1].bitcast(FP8X4), scales=h_scales[:, c0:c1],
-                                  in_=h_il[:, c0 * PACK:c1 * PACK])
-
-        win_codes = keep.tile([P, TAPS, TOK], I32, name="win_codes", align_bytes=64)
-        win_scales = keep.tile([P, TAPS, TOK], U8, name="win_scales", align_bytes=64)
-        dx_scales = keep.tile([P, 3, B * YP * XX], U8, name="dx_scales", align_bytes=64)
-
-        def shift_scales():
-            rows = h_scales[:].rearrange("p (r j) -> p r j", j=XP)
-            for dx in range(3):
-                nc.vector.tensor_copy(out=dx_scales[:, dx, :].rearrange("p (r j) -> p r j", j=XX), in_=rows[:, :, dx:dx + XX])
-
-        def window_scales(dy):
-            src = dx_scales[:].rearrange("p d n -> p (d n)").bitcast(I32).rearrange("p (q w) -> p q w", w=YP * XX // 4)
-            dst = win_scales[:, 3 * dy:3 * dy + 3, :].rearrange("p d n -> p (d n)").bitcast(I32)
-            nc.vector.tensor_copy(out=dst.rearrange("p (q w) -> p q w", w=POS // 4),
-                                  in_=src[:, :, dy * XX // 4:dy * XX // 4 + POS // 4])
-
-        def window_codes(tap):
-            dy, dx = tap // 3, tap % 3
-            src = h_codes[:].rearrange("p (b i j) -> p b i j", i=YP, j=XP)
-            nc.vector.tensor_copy(out=win_codes[:, tap, :].rearrange("p (b i j) -> p b i j", i=YY, j=XX),
-                                  in_=src[:, :, dy:dy + YY, dx:dx + XX])
-
-        quantised = {}
-
-        def quantise(j, i):
-            codes = work.tile([P, F], I32, name="codes", tag="codes", bufs=6, align_bytes=64)
-            scales = work.tile([P, F], U8, name="scales", tag="scales", bufs=6, align_bytes=64)
+        def quantise_strip(j, i):
+            codes = work.tile([P, F], I32, name="codes", tag="codes", bufs=CODE_BUFS, align_bytes=64)
+            scales = work.tile([P, F], U8, name="scales", tag="scales", bufs=CODE_BUFS, align_bytes=64)
             nc.vector.quantize_mx(out=codes[:].bitcast(FP8X4), scales=scales[:],
-                                  in_=il[j][:, i * F:(i + 1) * F, :].rearrange("p n t -> p (n t)"))
+                                  in_=interleaved[j][:, i * F:(i + 1) * F, :].rearrange("p n t -> p (n t)"))
             quantised[j, i] = (codes, scales)
-
-        def multiply(j):
-            for i in range(len(GROUPS[j])):
-                if GROUPS[j][i][1] < TAPS - 1:
-                    multiply_strip(j, i)
 
         def multiply_strip(j, i):
             gate, tap = GROUPS[j][i]
             codes, scales = quantised[j, i]
             for m in range(MT):
                 if tap == 0:
-                    acc[gate, m] = psum.tile([P, F], F32, name="acc", tag="acc", bufs=6)
-                nc.tensor.matmul_mx(out=acc[gate, m][:], lhsT=win_codes[:, tap, m * P:(m + 1) * P].bitcast(FP8X4),
-                                    lhsT_scale=win_scales[:, tap, m * P:(m + 1) * P],
+                    sums[gate, m] = psum.tile([P, F], F32, name="sum", tag="sum", bufs=SUM_BANKS)
+                tokens = slice(m * P, (m + 1) * P)
+                nc.tensor.matmul_mx(out=sums[gate, m][:], lhsT=win_codes[:, tap, tokens].bitcast(FP8X4),
+                                    lhsT_scale=win_scales[:, tap, tokens],
                                     rhs=codes[:].bitcast(FP8X4), rhs_scale=scales[:],
                                     start=(tap == 0), stop=(tap == TAPS - 1))
 
-        wo_il = keep.tile([P, E, PACK], BF16, name="wo_il", align_bytes=64)
+        h_interleaved = keep.tile([P, HALO * PACK], BF16, name="h_interleaved", align_bytes=64)
+        h_codes = keep.tile([P, HALO], I32, name="h_codes", align_bytes=64)
+
+        def turn_words(bank, rows):
+            words = rows.bitcast(F32)
+            for u in range(2):
+                nc.tensor.transpose(bank[:, u, :], words[:, u:F // 2:2], ident_f32[:])
+
+        def turn_h(i):
+            m0, n = h_pieces[i]
+            bank = psum.tile([P, 2, 2, P], F32, name="turn", tag="turn", bufs=TURN_BANKS)
+            for m in range(n):
+                turn_words(bank[:, m, :, :], h_raw[i][:, m, :])
+            dst = h_interleaved[:, m0 * P * PACK:(m0 + n) * P * PACK].bitcast(F32).rearrange("p (m r u) -> p m r u", m=n, u=2)
+            nc.vector.tensor_copy(out=dst, in_=bank[:, 0:n, :, :].rearrange("p m u r -> p m r u"))
+
+        def quantise_h(c0, c1):
+            nc.vector.quantize_mx(out=h_codes[:, c0:c1].bitcast(FP8X4), scales=h_scales[:, c0:c1],
+                                  in_=h_interleaved[:, c0 * PACK:c1 * PACK])
+
+        win_codes = keep.tile([P, TAPS, TOK], I32, name="win_codes", align_bytes=64)
+        win_scales = keep.tile([P, TAPS, TOK], U8, name="win_scales", align_bytes=64)
+        dx_scales = keep.tile([P, SIDE, B * YP * XX], U8, name="dx_scales", align_bytes=64)
+        row_words = XX // 4
+
+        def shift_scales():
+            rows = h_scales[:].rearrange("p (r j) -> p r j", j=XP)
+            for dx in range(SIDE):
+                nc.vector.tensor_copy(out=dx_scales[:, dx, :].rearrange("p (r j) -> p r j", j=XX), in_=rows[:, :, dx:dx + XX])
+
+        def window_scales(dy):
+            src = dx_scales[:].rearrange("p d n -> p (d n)").bitcast(I32).rearrange("p (q w) -> p q w", w=YP * row_words)
+            dst = win_scales[:, SIDE * dy:SIDE * (dy + 1), :].rearrange("p d n -> p (d n)").bitcast(I32)
+            nc.vector.tensor_copy(out=dst.rearrange("p (q w) -> p q w", w=YY * row_words),
+                                  in_=src[:, :, dy * row_words:(dy + YY) * row_words])
+
+        def window_codes(tap):
+            dy, dx = tap // SIDE, tap % SIDE
+            src = h_codes[:].rearrange("p (b i j) -> p b i j", i=YP, j=XP)
+            nc.vector.tensor_copy(out=win_codes[:, tap, :].rearrange("p (b i j) -> p b i j", i=YY, j=XX),
+                                  in_=src[:, :, dy:dy + YY, dx:dx + XX])
+
+        wo_interleaved = keep.tile([P, E, PACK], BF16, name="wo_interleaved", align_bytes=64)
         wo_codes = keep.tile([P, E], I32, name="wo_codes", align_bytes=64)
         wo_scales = keep.tile([P, E], U8, name="wo_scales", align_bytes=64)
-
         wo_banks = {}
 
-        def wo_tensor(half):
-            wo_banks[half] = tensor_interleave(wo_raw[:, :, half * F:(half + 1) * F], F)
+        def wo_into_bank(q):
+            src = wo_planes[:, :, q * BANK_COLUMNS:(q + 1) * BANK_COLUMNS]
+            wo_banks[q] = interleave_into_bank(src, "sum", SUM_BANKS) if q < MT else interleave_into_bank(src, "turn", TURN_BANKS)
 
-        def wo_scalar(half):
-            empty_banks(wo_il[:, half * F:(half + 1) * F, :], wo_banks[half])
-
-        def wo_quantise(half):
+        def quantise_wo(half):
             cols = slice(half * F, (half + 1) * F)
             nc.vector.quantize_mx(out=wo_codes[:, cols].bitcast(FP8X4), scales=wo_scales[:, cols],
-                                  in_=wo_il[:, cols, :].rearrange("p n t -> p (n t)"))
+                                  in_=wo_interleaved[:, cols, :].rearrange("p n t -> p (n t)"))
 
-        gate_in = keep.tile([P, MT, F], F32, name="gate_in")
+        gate_sb = keep.tile([P, MT, F], F32, name="gate_sb")
         kept = keep.tile([P, MT, F], F32, name="kept")
-        cand = keep.tile([P, MT, F], F32, name="cand")
+        factor = keep.tile([P, MT, F], F32, name="factor")
         c_new = keep.tile([P, MT, F], F32, name="c_new")
         c_half = keep.tile([P, MT, F], BF16, name="c_half")
-
-        def flat(t):
-            return t[:].rearrange("p m f -> p (m f)")
-
-        def peep_f_term():
-            nc.vector.tensor_tensor(out=flat(gate_in), in0=flat(pf_sb), in1=flat(c_sb), op=ALU.mult)
-
-        def halve_c():
-            nc.vector.tensor_scalar(out=flat(c_half), in0=flat(c_sb), scalar1=0.5, scalar2=None, op0=ALU.mult)
-
-        def add_pre(gate, m):
-            nc.vector.tensor_tensor(out=gate_in[:, m, :], in0=acc[gate, m][:], in1=gate_in[:, m, :], op=ALU.add)
-
-        def tanh_f():
-            nc.scalar.activation(out=flat(gate_in), in_=flat(gate_in), func=ACT.Tanh, scale=0.5)
-
-        def keep_term():
-            nc.vector.scalar_tensor_tensor(out=flat(kept), in0=flat(gate_in), scalar=1.0, in1=flat(c_half), op0=ALU.add, op1=ALU.mult)
-
-        def tanh_g(m):
-            nc.scalar.activation(out=cand[:, m, :], in_=acc[1, m][:], func=ACT.Tanh)
-
+        hg = keep.tile([P, MT, F], BF16, name="hg")
         c_rows = out_1.rearrange("b i j f -> (b i j) f")
+        y_rows = out_0.rearrange("b i j e -> (b i j) e")
 
-        def cand_term(m):
-            nc.vector.scalar_tensor_tensor(out=cand[:, m, :], in0=gate_in[:, m, :], scalar=-1.0, in1=cand[:, m, :], op0=ALU.add, op1=ALU.mult)
+        def flat(tile):
+            return tile[:].rearrange("p m f -> p (m f)")
+
+        def add_sums(gate, m):
+            nc.vector.tensor_tensor(out=gate_sb[:, m, :], in0=sums[gate, m][:], in1=gate_sb[:, m, :], op=ALU.add)
+
+        def forget_gate_on_vector(stage):
+            if stage == 0:
+                nc.vector.tensor_tensor(out=flat(gate_sb), in0=flat(peep_f_sb), in1=flat(c_sb), op=ALU.mult)
+            if stage == 1:
+                nc.vector.tensor_scalar(out=flat(c_half), in0=flat(c_sb), scalar1=0.5, scalar2=None, op0=ALU.mult)
+            if stage == 2:
+                for m in range(MT):
+                    add_sums(GATE_F, m)
+            if stage == 4:
+                nc.vector.scalar_tensor_tensor(out=flat(kept), in0=flat(gate_sb), scalar=1.0, in1=flat(c_half),
+                                               op0=ALU.add, op1=ALU.mult)
+
+        def candidate(m):
+            nc.vector.scalar_tensor_tensor(out=factor[:, m, :], in0=gate_sb[:, m, :], scalar=-1.0, in1=factor[:, m, :],
+                                           op0=ALU.add, op1=ALU.mult)
 
         def cell(m):
-            nc.vector.scalar_tensor_tensor(out=c_new[:, m, :], in0=cand[:, m, :], scalar=-0.5, in1=kept[:, m, :], op0=ALU.mult, op1=ALU.add)
+            nc.vector.scalar_tensor_tensor(out=c_new[:, m, :], in0=factor[:, m, :], scalar=-0.5, in1=kept[:, m, :],
+                                           op0=ALU.mult, op1=ALU.add)
             nc.sync.dma_start(out=c_rows[m * P:(m + 1) * P, :], in_=c_new[:, m, :])
 
-        def peep_o_term(m):
-            nc.vector.tensor_tensor(out=gate_in[:, m, :], in0=c_new[:, m, :], in1=po_sb[:, m, :], op=ALU.mult)
+        def peephole_o(m):
+            nc.vector.tensor_tensor(out=gate_sb[:, m, :], in0=c_new[:, m, :], in1=peep_o_sb[:, m, :], op=ALU.mult)
 
-        def tanh_c(m):
-            nc.scalar.activation(out=cand[:, m, :], in_=c_new[:, m, :], func=ACT.Tanh)
+        def apply_gain(m):
+            nc.vector.scalar_tensor_tensor(out=factor[:, m, :], in0=factor[:, m, :], scalar=0.5, in1=gain_sb[:],
+                                           op0=ALU.mult, op1=ALU.mult)
 
-        def gain_term(m):
-            nc.vector.scalar_tensor_tensor(out=cand[:, m, :], in0=cand[:, m, :], scalar=0.5, in1=gain_sb[:], op0=ALU.mult, op1=ALU.mult)
-
-        def add_f():
-            for m in range(MT):
-                add_pre(0, m)
-
-        y_rows = out_0.rearrange("b i j e -> (b i j) e")
-        hg = keep.tile([P, MT, F], BF16, name="hg")
-        hg_il = {}
-        y_ps = {}
-
-        def gate_o(m):
-            add_pre(2, m)
-            nc.scalar.activation(out=gate_in[:, m, :], in_=gate_in[:, m, :], func=ACT.Tanh, scale=0.5)
-
-        def hidden(m):
-            nc.vector.scalar_tensor_tensor(out=hg[:, m, :], in0=gate_in[:, m, :], scalar=1.0, in1=cand[:, m, :], op0=ALU.add, op1=ALU.mult)
-            tp = psum.tile([P, 2, P], F32, name="tp", tag="tp", bufs=2)
-            words = hg[:, m, :].bitcast(F32)
-            for u in range(2):
-                nc.tensor.transpose(tp[:, u, :], words[:, u:F // 2:2], ident[:])
-            hg_il[m] = keep.tile([P, P * PACK], BF16, name="hg_il%d" % m, align_bytes=64)
-            nc.scalar.copy(out=hg_il[m][:].bitcast(F32).rearrange("p (r u) -> p r u", u=2), in_=tp[:].rearrange("p u r -> p r u"))
-
-        hg_q = {}
-
-        def hidden_quantise(m):
-            codes = keep.tile([P, P], I32, name="hg_codes%d" % m, align_bytes=64)
-            scales = keep.tile([P, P], U8, name="hg_scales%d" % m, align_bytes=64)
-            nc.vector.quantize_mx(out=codes[:].bitcast(FP8X4), scales=scales[:], in_=hg_il[m][:])
-            hg_q[m] = (codes, scales)
-
-        def project(m, half):
-            codes, scales = hg_q[m]
-            cols = slice(half * F, (half + 1) * F)
-            y_ps[m, half] = psum.tile([P, F], F32, name="acc", tag="acc", bufs=6)
-            nc.tensor.matmul_mx(out=y_ps[m, half][:], lhsT=codes[:].bitcast(FP8X4), lhsT_scale=scales[:],
-                                rhs=wo_codes[:, cols].bitcast(FP8X4), rhs_scale=wo_scales[:, cols], start=True, stop=True)
-
-        def store(m, half, on_scalar):
-            y_sb = keep.tile([P, F], F32, name="y_sb%d_%d" % (m, half))
-            if on_scalar:
-                nc.scalar.copy(out=y_sb[:], in_=y_ps[m, half][:])
-            else:
-                nc.vector.tensor_copy(out=y_sb[:], in_=y_ps[m, half][:])
-            nc.sync.dma_start(out=y_rows[m * P:(m + 1) * P, half * F:(half + 1) * F], in_=y_sb[:])
-
-        vector_steps = {5: [peep_f_term], 6: [halve_c], 7: [add_f], 9: [keep_term], 12: [lambda: cell(0), lambda: cell(1)], 13: [lambda: gain_term(0)], 14: [lambda: gain_term(1), lambda: peep_o_term(1)], 15: [lambda: gain_term(2), lambda: peep_o_term(2)]}
-        scalar_steps = {8: [tanh_f], 11: [lambda: tanh_g(0), lambda: tanh_g(1), lambda: tanh_g(2)], 13: [lambda: tanh_c(0), lambda: tanh_c(1), lambda: tanh_c(2)]}
-        late_steps = {13: [lambda: wo_tensor(0)], 14: [lambda: wo_scalar(0)]}
-        after_steps = {11: [lambda: cand_term(0), lambda: cand_term(1), lambda: cand_term(2)], 14: [lambda: multiply(14), lambda: wo_tensor(1), lambda: wo_scalar(1), lambda: early.add(14)]}
-        middle_steps = {12: [lambda: cell(2)], 13: [lambda: peep_o_term(0)]}
-        early = set()
-        last = len(GROUPS) - 1
-        widen_vector(0)
-        widen_scalar(1, range(PACK))
-        interleave_vector(0)
+        widen_on_vector(0)
+        widen_on_scalar(1, range(PACK))
+        interleave_by_copy(0)
         turn_h(0)
-        quantise(0, 0)
+        quantise_strip(0, 0)
         turn_h(1)
         turn_h(2)
         quantise_h(0, F)
         quantise_h(F, HALO)
-        interleave_vector(1)
+        interleave_by_copy(1)
         shift_scales()
         window_codes(0)
         window_scales(0)
+
         for j in range(1, len(GROUPS)):
-            if j < last:
-                widen_scalar(j + 1, range(0, 2))
+            f_stage, cell_stage = j - F_END, j - G_END
+            n = group_columns(j)
+            if j < LAST:
+                widen_on_scalar(j + 1, range(PACK - 1))
+            if tensor_columns(j):
+                empty_bank(interleaved_tile(j)[:, n - BANK_COLUMNS:n, :], banks[j])
+            if f_stage == 3:
+                nc.scalar.activation(out=flat(gate_sb), in_=flat(gate_sb), func=ACT.Tanh, scale=0.5)
+            for m in range(MT):
+                if cell_stage == 1:
+                    nc.scalar.activation(out=factor[:, m, :], in_=sums[GATE_G, m][:], func=ACT.Tanh)
+                if cell_stage == 3:
+                    nc.scalar.activation(out=factor[:, m, :], in_=c_new[:, m, :], func=ACT.Tanh)
+            if j < LAST:
+                widen_on_scalar(j + 1, [PACK - 1])
+
             if j > 1:
-                interleave_scalar(j)
-            for step in scalar_steps.get(j, []):
-                step()
-            if j < last:
-                widen_scalar(j + 1, range(2, PACK))
-            if j > 1:
-                interleave_vector(j)
-            if j + 2 <= last:
-                widen_vector(j + 2)
+                interleave_by_copy(j)
+            if j + 2 <= LAST:
+                widen_on_vector(j + 2)
             for gate, tap in GROUPS[j]:
-                if gate == 0:
+                if gate == GATE_F:
                     window_codes(tap)
-                    if tap % 3 == 0:
-                        window_scales(tap // 3)
-            for step in vector_steps.get(j, []):
-                step()
-            if j < last:
-                interleave_tensor(j + 1)
-            for step in late_steps.get(j, []):
-                step()
-            if j - 1 not in early:
-                multiply(j - 1)
+                    if tap % SIDE == 0:
+                        window_scales(tap // SIDE)
+            forget_gate_on_vector(f_stage)
+            if cell_stage == 2:
+                cell(0)
+                cell(1)
+            if cell_stage == 3:
+                peephole_o(0)
+            if cell_stage == 4:
+                apply_gain(0)
+                apply_gain(1)
+            if cell_stage == 5:
+                apply_gain(2)
+
+            if j < LAST and tensor_columns(j + 1):
+                n_next = group_columns(j + 1)
+                banks[j + 1] = interleave_into_bank(planes[j + 1][:, :, n_next - BANK_COLUMNS:n_next], "turn", TURN_BANKS)
+            if 1 <= cell_stage <= MT:
+                wo_into_bank(cell_stage - 1)
+            if cell_stage == MT:
+                wo_into_bank(MT)
+            if j <= PROMPT_FROM:
+                for i in range(len(GROUPS[j - 1])):
+                    multiply_strip(j - 1, i)
             for i in range(len(GROUPS[j])):
-                quantise(j, i)
-                if GROUPS[j][i][1] == TAPS - 1:
-                    if i > 0:
-                        multiply(j)
-                        early.add(j)
+                quantise_strip(j, i)
+                if j >= PROMPT_FROM:
                     multiply_strip(j, i)
-                if i == 0:
-                    for step in middle_steps.get(j, []):
-                        step()
-            for step in after_steps.get(j, []):
-                step()
-        wo_quantise(0)
-        gate_o(0)
-        gate_o(1)
-        gate_o(2)
-        hidden(0)
-        hidden(1)
-        hidden(2)
-        hidden_quantise(0)
+                if i == 0 and cell_stage == 2:
+                    cell(2)
+                if i == 0 and cell_stage == 3:
+                    peephole_o(1)
+            if cell_stage == 1:
+                for m in range(MT):
+                    candidate(m)
+
+        hg_interleaved, hg_quantised, y_banks = {}, {}, {}
+
+        def quantise_hg(m):
+            codes = keep.tile([P, P], I32, name="hg_codes%d" % m, align_bytes=64)
+            scales = keep.tile([P, P], U8, name="hg_scales%d" % m, align_bytes=64)
+            nc.vector.quantize_mx(out=codes[:].bitcast(FP8X4), scales=scales[:], in_=hg_interleaved[m][:])
+            hg_quantised[m] = (codes, scales)
+
+        def project(m, half):
+            codes, scales = hg_quantised[m]
+            cols = slice(half * F, (half + 1) * F)
+            y_banks[m, half] = psum.tile([P, F], F32, name="sum", tag="sum", bufs=SUM_BANKS)
+            nc.tensor.matmul_mx(out=y_banks[m, half][:], lhsT=codes[:].bitcast(FP8X4), lhsT_scale=scales[:],
+                                rhs=wo_codes[:, cols].bitcast(FP8X4), rhs_scale=wo_scales[:, cols], start=True, stop=True)
+
+        def store_y(m, half):
+            y_sb = keep.tile([P, F], F32, name="y_sb%d_%d" % (m, half))
+            if half == 0:
+                nc.scalar.copy(out=y_sb[:], in_=y_banks[m, half][:])
+            else:
+                nc.vector.tensor_copy(out=y_sb[:], in_=y_banks[m, half][:])
+            nc.sync.dma_start(out=y_rows[m * P:(m + 1) * P, half * F:(half + 1) * F], in_=y_sb[:])
+
+        for q in range(E // BANK_COLUMNS):
+            empty_bank(wo_interleaved[:, q * BANK_COLUMNS:(q + 1) * BANK_COLUMNS, :], wo_banks[q])
+        peephole_o(2)
+        for m in range(MT):
+            add_sums(GATE_O, m)
+            nc.scalar.activation(out=gate_sb[:, m, :], in_=gate_sb[:, m, :], func=ACT.Tanh, scale=0.5)
+        for m in range(MT):
+            nc.vector.scalar_tensor_tensor(out=hg[:, m, :], in0=gate_sb[:, m, :], scalar=1.0, in1=factor[:, m, :],
+                                           op0=ALU.add, op1=ALU.mult)
+            bank = psum.tile([P, 2, P], F32, name="turn", tag="turn", bufs=TURN_BANKS)
+            turn_words(bank[:], hg[:, m, :])
+            hg_interleaved[m] = keep.tile([P, P * PACK], BF16, name="hg_interleaved%d" % m, align_bytes=64)
+            nc.scalar.copy(out=hg_interleaved[m][:].bitcast(F32).rearrange("p (r u) -> p r u", u=2),
+                           in_=bank[:].rearrange("p u r -> p r u"))
+        quantise_wo(0)
+        quantise_hg(0)
         project(0, 0)
-        wo_quantise(1)
+        quantise_wo(1)
         project(0, 1)
-        hidden_quantise(1)
+        quantise_hg(1)
         project(1, 0)
         project(1, 1)
-        store(0, 0, True)
-        hidden_quantise(2)
+        store_y(0, 0)
+        quantise_hg(2)
         project(2, 0)
         project(2, 1)
-        store(0, 1, False)
-        store(1, 0, True)
-        store(1, 1, False)
-        store(2, 0, True)
-        store(2, 1, False)
+        store_y(0, 1)
+        for m in range(1, MT):
+            store_y(m, 0)
+            store_y(m, 1)

from contextlib import ExitStack

import concourse.mybir as mybir
from concourse.masks import make_identity

F32 = mybir.dt.float32
BF16 = mybir.dt.bfloat16
I32 = mybir.dt.int32
U8 = mybir.dt.uint8
FP8 = mybir.dt.float8_e4m3fn
FP8X4 = mybir.dt.float8_e4m3fn_x4
ACT = mybir.ActivationFunctionType
ALU = mybir.AluOpType

B, YY, XX, F, E = 8, 6, 8, 512, 1024
SIDE = 3
TAPS = SIDE * SIDE
YP, XP = YY + SIDE - 1, XX + SIDE - 1
P = 128
PACK = 4
POS = YY * XX
TOK = B * POS
MT = TOK // P
HALO = B * YP * XP
HT = HALO // P
GATE_F, GATE_G, GATE_O = 0, 1, 2
BANK_COLUMNS = 256

FLOPS = 2 * TOK * F * (TAPS * 3 * F + E)

STRIPS = [(gate, tap) for gate in (GATE_F, GATE_G, GATE_O) for tap in range(TAPS)]
SINGLES_FIRST, SINGLES_LAST = 3, 2
GROUPS = (
    [STRIPS[s:s + 1] for s in range(SINGLES_FIRST)]
    + [STRIPS[s:s + 2] for s in range(SINGLES_FIRST, len(STRIPS) - SINGLES_LAST, 2)]
    + [STRIPS[s:s + 1] for s in range(len(STRIPS) - SINGLES_LAST, len(STRIPS))]
)
LAST = len(GROUPS) - 1
F_END = [j for j, g in enumerate(GROUPS) if (GATE_F, TAPS - 1) in g][0]
G_END = [j for j, g in enumerate(GROUPS) if (GATE_G, TAPS - 1) in g][0]

VECTOR_SHARE = 896
VECTOR_SHARE_LATE = 2 * F
PROMPT_FROM = 4
PLANE_BUFS, INTERLEAVED_BUFS, CODE_BUFS = 4, 3, 6
SUM_BANKS, TURN_BANKS = 2 * MT, 2


def group_columns(j):
    return len(GROUPS[j]) * F


def vector_widens(j, t):
    if j == 0:
        return F
    if len(GROUPS[j]) == 1 or t < PACK - 1:
        return 0
    return VECTOR_SHARE if j <= G_END else VECTOR_SHARE_LATE


def tensor_columns(j):
    return BANK_COLUMNS if 2 <= j <= LAST - SINGLES_LAST else 0


def interleave_views(dst, src):
    return dst.rearrange("p (c i) t -> p c t i", i=4), src.rearrange("p t (c i) -> p c t i", i=4)


def tile_peepholeconvlstmninetap_kernel(tc, h, c, wh_bytes, wh_scale, peep_f, peep_o, gain, wo, out_0, out_1):
    nc = tc.nc
    with ExitStack() as ctx:
        keep = ctx.enter_context(tc.tile_pool(name="keep", bufs=1))
        work = ctx.enter_context(tc.tile_pool(name="work", bufs=INTERLEAVED_BUFS))
        psum = ctx.enter_context(tc.psum_pool(name="psum", bufs=1))
        ctx.enter_context(tc.manual_schedule())

        wscale = keep.tile([P, PACK], F32, name="wscale")
        nc.sync.dma_start(out=wscale[:], in_=wh_scale.rearrange("a b (p t) o -> p (a b t o)", t=PACK))
        wbytes = [keep.tile([P, PACK, group_columns(j)], U8, name="wbytes%d" % j) for j in range(len(GROUPS))]

        def load_w(j, t0=0, t1=PACK):
            for i, (gate, tap) in enumerate(GROUPS[j]):
                src = wh_bytes[tap // SIDE, tap % SIDE].rearrange("(p t) n -> p t n", t=PACK)
                nc.sync.dma_start(out=wbytes[j][:, t0:t1, i * F:(i + 1) * F], in_=src[:, t0:t1, gate * F:(gate + 1) * F])

        def load_peephole(dst, src):
            rows = src.rearrange("i j f -> (i j) f")
            for m in range(MT):
                p0 = 0
                while p0 < P:
                    r0 = (m * P + p0) % POS
                    n = min(POS - r0, P - p0)
                    nc.sync.dma_start(out=dst[p0:p0 + n, m, :], in_=rows[r0:r0 + n, :])
                    p0 = p0 + n

        h_rows = h.rearrange("b i j f -> (b i j) f").rearrange("(m p) f -> p m f", p=P)
        h_pieces = [(m0, min(2, HT - m0)) for m0 in range(0, HT, 2)]
        h_raw = [keep.tile([P, n, F], BF16, name="h_raw%d" % m0) for m0, n in h_pieces]

        def load_h(i):
            m0, n = h_pieces[i]
            nc.sync.dma_start(out=h_raw[i][:], in_=h_rows[:, m0:m0 + n, :])

        for t0 in (0, PACK // 2):
            load_w(1, t0, t0 + PACK // 2)
            load_w(0, t0, t0 + PACK // 2)
        load_h(0)
        load_w(2)
        load_h(1)
        load_h(2)
        for j in range(SINGLES_FIRST, F_END + 2):
            load_w(j)
        c_sb = keep.tile([P, MT, F], BF16, name="c_sb")
        nc.sync.dma_start(out=c_sb[:], in_=c.rearrange("b i j f -> (b i j) f").rearrange("(m p) f -> p m f", p=P))
        peep_f_sb = keep.tile([P, MT, F], BF16, name="peep_f_sb")
        load_peephole(peep_f_sb, peep_f)
        for j in range(F_END + 2, G_END + 2):
            load_w(j)
        gain_sb = keep.tile([P, F], BF16, name="gain_sb")
        nc.sync.dma_start(out=gain_sb[:], in_=gain.partition_broadcast(P))
        peep_o_sb = keep.tile([P, MT, F], BF16, name="peep_o_sb")
        load_peephole(peep_o_sb, peep_o)
        for j in range(G_END + 2, len(GROUPS)):
            load_w(j)
        wo_planes = keep.tile([P, PACK, E], BF16, name="wo_planes")
        nc.sync.dma_start(out=wo_planes[:], in_=wo.rearrange("(p t) e -> p t e", t=PACK))

        ident_f32 = keep.tile([P, P], F32, name="ident_f32")
        make_identity(nc, ident_f32[:])
        ident_bf16 = keep.tile([P, P], BF16, name="ident_bf16")
        make_identity(nc, ident_bf16[:])
        h_scales = keep.tile([P, HALO], U8, name="h_scales", align_bytes=64)
        nc.vector.memset(h_scales[:].bitcast(I32), 0)

        planes, interleaved, banks, quantised, sums = {}, {}, {}, {}, {}

        def plane_tile(j):
            if j not in planes:
                planes[j] = work.tile([P, PACK, group_columns(j)], BF16, name="planes", tag="planes", bufs=PLANE_BUFS)
            return planes[j]

        def interleaved_tile(j):
            if j not in interleaved:
                interleaved[j] = work.tile([P, group_columns(j), PACK], BF16, name="interleaved", tag="interleaved",
                                           bufs=INTERLEAVED_BUFS, align_bytes=64)
            return interleaved[j]

        def widen_on_vector(j):
            for t in range(PACK):
                x = vector_widens(j, t)
                if x > 0:
                    nc.vector.tensor_scalar(out=plane_tile(j)[:, t, 0:x], in0=wbytes[j][:, t, 0:x].bitcast(FP8),
                                            scalar1=wscale[:, t:t + 1], scalar2=None, op0=ALU.mult)

        def widen_on_scalar(j, ts):
            n = group_columns(j)
            for t in ts:
                x = vector_widens(j, t)
                if x < n:
                    nc.scalar.activation(out=plane_tile(j)[:, t, x:n], in_=wbytes[j][:, t, x:n].bitcast(FP8),
                                         func=ACT.Copy, scale=wscale[:, t:t + 1])

        def interleave_into_bank(src, tag, bufs):
            bank = psum.tile([P, BANK_COLUMNS * PACK], BF16, name=tag, tag=tag, bufs=bufs)
            for c0 in range(0, BANK_COLUMNS, P):
                nc.tensor.matmul(out=bank[:, c0 * PACK:(c0 + P) * PACK], lhsT=ident_bf16[:],
                                 rhs=src[:, :, c0:c0 + P].rearrange("p t n -> p n t"), start=True, stop=True)
            return bank

        def empty_bank(dst, bank):
            nc.scalar.copy(out=dst.rearrange("p n t -> p (n t)"), in_=bank[:])

        def interleave_by_copy(j):
            n = group_columns(j) - tensor_columns(j)
            dst, src = interleave_views(interleaved_tile(j)[:, 0:n, :], planes[j][:, :, 0:n])
            if j == LAST:
                nc.scalar.copy(out=dst, in_=src)
            else:
                nc.vector.tensor_copy(out=dst, in_=src)

        def quantise_strip(j, i):
            codes = work.tile([P, F], I32, name="codes", tag="codes", bufs=CODE_BUFS, align_bytes=64)
            scales = work.tile([P, F], U8, name="scales", tag="scales", bufs=CODE_BUFS, align_bytes=64)
            nc.vector.quantize_mx(out=codes[:].bitcast(FP8X4), scales=scales[:],
                                  in_=interleaved[j][:, i * F:(i + 1) * F, :].rearrange("p n t -> p (n t)"))
            quantised[j, i] = (codes, scales)

        def multiply_strip(j, i):
            gate, tap = GROUPS[j][i]
            codes, scales = quantised[j, i]
            for m in range(MT):
                if tap == 0:
                    sums[gate, m] = psum.tile([P, F], F32, name="sum", tag="sum", bufs=SUM_BANKS)
                tokens = slice(m * P, (m + 1) * P)
                nc.tensor.matmul_mx(out=sums[gate, m][:], lhsT=win_codes[:, tap, tokens].bitcast(FP8X4),
                                    lhsT_scale=win_scales[:, tap, tokens],
                                    rhs=codes[:].bitcast(FP8X4), rhs_scale=scales[:],
                                    start=(tap == 0), stop=(tap == TAPS - 1))

        h_interleaved = keep.tile([P, HALO * PACK], BF16, name="h_interleaved", align_bytes=64)
        h_codes = keep.tile([P, HALO], I32, name="h_codes", align_bytes=64)

        def turn_words(bank, rows):
            words = rows.bitcast(F32)
            for u in range(2):
                nc.tensor.transpose(bank[:, u, :], words[:, u:F // 2:2], ident_f32[:])

        def turn_h(i):
            m0, n = h_pieces[i]
            bank = psum.tile([P, 2, 2, P], F32, name="turn", tag="turn", bufs=TURN_BANKS)
            for m in range(n):
                turn_words(bank[:, m, :, :], h_raw[i][:, m, :])
            dst = h_interleaved[:, m0 * P * PACK:(m0 + n) * P * PACK].bitcast(F32).rearrange("p (m r u) -> p m r u", m=n, u=2)
            nc.vector.tensor_copy(out=dst, in_=bank[:, 0:n, :, :].rearrange("p m u r -> p m r u"))

        def quantise_h(c0, c1):
            nc.vector.quantize_mx(out=h_codes[:, c0:c1].bitcast(FP8X4), scales=h_scales[:, c0:c1],
                                  in_=h_interleaved[:, c0 * PACK:c1 * PACK])

        win_codes = keep.tile([P, TAPS, TOK], I32, name="win_codes", align_bytes=64)
        win_scales = keep.tile([P, TAPS, TOK], U8, name="win_scales", align_bytes=64)
        dx_scales = keep.tile([P, SIDE, B * YP * XX], U8, name="dx_scales", align_bytes=64)
        row_words = XX // 4

        def shift_scales():
            rows = h_scales[:].rearrange("p (r j) -> p r j", j=XP)
            for dx in range(SIDE):
                nc.vector.tensor_copy(out=dx_scales[:, dx, :].rearrange("p (r j) -> p r j", j=XX), in_=rows[:, :, dx:dx + XX])

        def window_scales(dy):
            src = dx_scales[:].rearrange("p d n -> p (d n)").bitcast(I32).rearrange("p (q w) -> p q w", w=YP * row_words)
            dst = win_scales[:, SIDE * dy:SIDE * (dy + 1), :].rearrange("p d n -> p (d n)").bitcast(I32)
            nc.vector.tensor_copy(out=dst.rearrange("p (q w) -> p q w", w=YY * row_words),
                                  in_=src[:, :, dy * row_words:(dy + YY) * row_words])

        def window_codes(tap):
            dy, dx = tap // SIDE, tap % SIDE
            src = h_codes[:].rearrange("p (b i j) -> p b i j", i=YP, j=XP)
            nc.vector.tensor_copy(out=win_codes[:, tap, :].rearrange("p (b i j) -> p b i j", i=YY, j=XX),
                                  in_=src[:, :, dy:dy + YY, dx:dx + XX])

        wo_interleaved = keep.tile([P, E, PACK], BF16, name="wo_interleaved", align_bytes=64)
        wo_codes = keep.tile([P, E], I32, name="wo_codes", align_bytes=64)
        wo_scales = keep.tile([P, E], U8, name="wo_scales", align_bytes=64)
        wo_banks = {}

        def wo_into_bank(q):
            src = wo_planes[:, :, q * BANK_COLUMNS:(q + 1) * BANK_COLUMNS]
            wo_banks[q] = interleave_into_bank(src, "sum", SUM_BANKS) if q < MT else interleave_into_bank(src, "turn", TURN_BANKS)

        def quantise_wo(half):
            cols = slice(half * F, (half + 1) * F)
            nc.vector.quantize_mx(out=wo_codes[:, cols].bitcast(FP8X4), scales=wo_scales[:, cols],
                                  in_=wo_interleaved[:, cols, :].rearrange("p n t -> p (n t)"))

        gate_sb = keep.tile([P, MT, F], F32, name="gate_sb")
        kept = keep.tile([P, MT, F], F32, name="kept")
        factor = keep.tile([P, MT, F], F32, name="factor")
        c_new = keep.tile([P, MT, F], F32, name="c_new")
        c_half = keep.tile([P, MT, F], BF16, name="c_half")
        hg = keep.tile([P, MT, F], BF16, name="hg")
        c_rows = out_1.rearrange("b i j f -> (b i j) f")
        y_rows = out_0.rearrange("b i j e -> (b i j) e")

        def flat(tile):
            return tile[:].rearrange("p m f -> p (m f)")

        def add_sums(gate, m):
            nc.vector.tensor_tensor(out=gate_sb[:, m, :], in0=sums[gate, m][:], in1=gate_sb[:, m, :], op=ALU.add)

        def forget_gate_on_vector(stage):
            if stage == 0:
                nc.vector.tensor_tensor(out=flat(gate_sb), in0=flat(peep_f_sb), in1=flat(c_sb), op=ALU.mult)
            if stage == 1:
                nc.vector.tensor_scalar(out=flat(c_half), in0=flat(c_sb), scalar1=0.5, scalar2=None, op0=ALU.mult)
            if stage == 2:
                for m in range(MT):
                    add_sums(GATE_F, m)
            if stage == 4:
                nc.vector.scalar_tensor_tensor(out=flat(kept), in0=flat(gate_sb), scalar=1.0, in1=flat(c_half),
                                               op0=ALU.add, op1=ALU.mult)

        def candidate(m):
            nc.vector.scalar_tensor_tensor(out=factor[:, m, :], in0=gate_sb[:, m, :], scalar=-1.0, in1=factor[:, m, :],
                                           op0=ALU.add, op1=ALU.mult)

        def cell(m):
            nc.vector.scalar_tensor_tensor(out=c_new[:, m, :], in0=factor[:, m, :], scalar=-0.5, in1=kept[:, m, :],
                                           op0=ALU.mult, op1=ALU.add)
            nc.sync.dma_start(out=c_rows[m * P:(m + 1) * P, :], in_=c_new[:, m, :])

        def peephole_o(m):
            nc.vector.tensor_tensor(out=gate_sb[:, m, :], in0=c_new[:, m, :], in1=peep_o_sb[:, m, :], op=ALU.mult)

        def apply_gain(m):
            nc.vector.scalar_tensor_tensor(out=factor[:, m, :], in0=factor[:, m, :], scalar=0.5, in1=gain_sb[:],
                                           op0=ALU.mult, op1=ALU.mult)

        widen_on_vector(0)
        widen_on_scalar(1, range(PACK))
        interleave_by_copy(0)
        turn_h(0)
        quantise_strip(0, 0)
        turn_h(1)
        turn_h(2)
        quantise_h(0, F)
        quantise_h(F, HALO)
        interleave_by_copy(1)
        shift_scales()
        window_codes(0)
        window_scales(0)

        for j in range(1, len(GROUPS)):
            f_stage, cell_stage = j - F_END, j - G_END
            n = group_columns(j)
            if j < LAST:
                widen_on_scalar(j + 1, range(PACK - 1))
            if tensor_columns(j):
                empty_bank(interleaved_tile(j)[:, n - BANK_COLUMNS:n, :], banks[j])
            if f_stage == 3:
                nc.scalar.activation(out=flat(gate_sb), in_=flat(gate_sb), func=ACT.Tanh, scale=0.5)
            for m in range(MT):
                if cell_stage == 1:
                    nc.scalar.activation(out=factor[:, m, :], in_=sums[GATE_G, m][:], func=ACT.Tanh)
                if cell_stage == 3:
                    nc.scalar.activation(out=factor[:, m, :], in_=c_new[:, m, :], func=ACT.Tanh)
            if j < LAST:
                widen_on_scalar(j + 1, [PACK - 1])

            if j > 1:
                interleave_by_copy(j)
            if j + 2 <= LAST:
                widen_on_vector(j + 2)
            for gate, tap in GROUPS[j]:
                if gate == GATE_F:
                    window_codes(tap)
                    if tap % SIDE == 0:
                        window_scales(tap // SIDE)
            forget_gate_on_vector(f_stage)
            if cell_stage == 2:
                cell(0)
                cell(1)
            if cell_stage == 3:
                peephole_o(0)
            if cell_stage == 4:
                apply_gain(0)
                apply_gain(1)
            if cell_stage == 5:
                apply_gain(2)

            if j < LAST and tensor_columns(j + 1):
                n_next = group_columns(j + 1)
                banks[j + 1] = interleave_into_bank(planes[j + 1][:, :, n_next - BANK_COLUMNS:n_next], "turn", TURN_BANKS)
            if 1 <= cell_stage <= MT:
                wo_into_bank(cell_stage - 1)
            if cell_stage == MT:
                wo_into_bank(MT)
            if j <= PROMPT_FROM:
                for i in range(len(GROUPS[j - 1])):
                    multiply_strip(j - 1, i)
            for i in range(len(GROUPS[j])):
                quantise_strip(j, i)
                if j >= PROMPT_FROM:
                    multiply_strip(j, i)
                if i == 0 and cell_stage == 2:
                    cell(2)
                if i == 0 and cell_stage == 3:
                    peephole_o(1)
            if cell_stage == 1:
                for m in range(MT):
                    candidate(m)

        hg_interleaved, hg_quantised, y_banks = {}, {}, {}

        def quantise_hg(m):
            codes = keep.tile([P, P], I32, name="hg_codes%d" % m, align_bytes=64)
            scales = keep.tile([P, P], U8, name="hg_scales%d" % m, align_bytes=64)
            nc.vector.quantize_mx(out=codes[:].bitcast(FP8X4), scales=scales[:], in_=hg_interleaved[m][:])
            hg_quantised[m] = (codes, scales)

        def project(m, half):
            codes, scales = hg_quantised[m]
            cols = slice(half * F, (half + 1) * F)
            y_banks[m, half] = psum.tile([P, F], F32, name="sum", tag="sum", bufs=SUM_BANKS)
            nc.tensor.matmul_mx(out=y_banks[m, half][:], lhsT=codes[:].bitcast(FP8X4), lhsT_scale=scales[:],
                                rhs=wo_codes[:, cols].bitcast(FP8X4), rhs_scale=wo_scales[:, cols], start=True, stop=True)

        def store_y(m, half):
            y_sb = keep.tile([P, F], F32, name="y_sb%d_%d" % (m, half))
            if half == 0:
                nc.scalar.copy(out=y_sb[:], in_=y_banks[m, half][:])
            else:
                nc.vector.tensor_copy(out=y_sb[:], in_=y_banks[m, half][:])
            nc.sync.dma_start(out=y_rows[m * P:(m + 1) * P, half * F:(half + 1) * F], in_=y_sb[:])

        for q in range(E // BANK_COLUMNS):
            empty_bank(wo_interleaved[:, q * BANK_COLUMNS:(q + 1) * BANK_COLUMNS, :], wo_banks[q])
        peephole_o(2)
        for m in range(MT):
            add_sums(GATE_O, m)
            nc.scalar.activation(out=gate_sb[:, m, :], in_=gate_sb[:, m, :], func=ACT.Tanh, scale=0.5)
        for m in range(MT):
            nc.vector.scalar_tensor_tensor(out=hg[:, m, :], in0=gate_sb[:, m, :], scalar=1.0, in1=factor[:, m, :],
                                           op0=ALU.add, op1=ALU.mult)
            bank = psum.tile([P, 2, P], F32, name="turn", tag="turn", bufs=TURN_BANKS)
            turn_words(bank[:], hg[:, m, :])
            hg_interleaved[m] = keep.tile([P, P * PACK], BF16, name="hg_interleaved%d" % m, align_bytes=64)
            nc.scalar.copy(out=hg_interleaved[m][:].bitcast(F32).rearrange("p (r u) -> p r u", u=2),
                           in_=bank[:].rearrange("p u r -> p r u"))
        quantise_wo(0)
        quantise_hg(0)
        project(0, 0)
        quantise_wo(1)
        project(0, 1)
        quantise_hg(1)
        project(1, 0)
        project(1, 1)
        store_y(0, 0)
        quantise_hg(2)
        project(2, 0)
        project(2, 1)
        store_y(0, 1)
        for m in range(1, MT):
            store_y(m, 0)
            store_y(m, 1)
